import numpy as np
import ml_dtypes


def mxq(x, axis, fmt="e4m3"):
    dtype, down = {"e4m3": (ml_dtypes.float8_e4m3fn, 7), "e5m2": (ml_dtypes.float8_e5m2, 14)}[fmt]
    v = np.moveaxis(np.asarray(x, np.float32).astype(ml_dtypes.bfloat16).astype(np.float64), axis, -1)
    blocks = v.reshape(v.shape[:-1] + (-1, 32))
    amax = np.abs(blocks).max(-1, keepdims=True)
    byte = np.maximum(np.where(amax > 0, np.frexp(amax)[1] - 1 + 127, 0) - down, 1)
    scale = np.exp2(byte - 127.0)
    codes = (blocks / scale).astype(np.float32).astype(dtype).astype(np.float64)
    return np.moveaxis((codes * scale).reshape(v.shape), -1, axis)


WIDE = False


def mx_kscale(k):
    if not WIDE:
        return np.ones(k)
    levels = np.array([10, -10, 5, -5, 0])
    if k % 512:
        return np.exp2(np.random.permutation(np.resize(levels, k // 32))).repeat(32)
    a = np.empty((k // 512, 16))
    for p in range(k // 512):
        a[p, :8] = np.random.permutation(np.resize(levels, 8))
        for g in range(8):
            far = levels[np.abs(levels - a[p, g]) >= 10]
            a[p, g + 8] = far[np.random.randint(len(far))]
    return np.exp2(a.ravel()).repeat(32)


def f64(x):
    return np.asarray(x).astype(np.float64)


def striped(idx):
    return np.tile(idx.reshape(-1, 16).T, (8, 1)).astype(np.uint16)


def unstriped(offs):
    return offs[:16].T.reshape(-1).astype(np.int64)


def pack_weight(w):
    k, n = w.shape
    w = f64(np.asarray(w, np.float32).astype(ml_dtypes.bfloat16)).reshape(k // 32, 32, n)
    amax = np.abs(w).max(1)
    byte = np.clip(np.where(amax > 0, np.frexp(amax)[1] - 1 + 127 - 7, 1), 1, 254)
    scaled = (w * np.exp2(127.0 - byte)[:, None, :]).reshape(k, n).astype(np.float32)
    words = np.ascontiguousarray(scaled.reshape(k // 512, 128, 4, n).transpose(0, 1, 3, 2)).astype(ml_dtypes.float8_e4m3fn).view(np.uint8)
    return words, np.ascontiguousarray(byte.astype(np.uint8).reshape(k // 512, 16, n))


def unpack_weight(words, scales):
    g, p, n, _ = words.shape
    vals = np.ascontiguousarray(words).view(ml_dtypes.float8_e4m3fn).astype(np.float64) * np.repeat(np.exp2(scales.astype(np.float64) - 127.0), 8, axis=1)[..., None]
    return vals.transpose(0, 1, 3, 2).reshape(g * 512, n)


K, T, S, H, N = 1024, 1024, 512, 512, 256


def setup_inputs():
    n = np.random.standard_normal
    s = mx_kscale(K)[:, None]
    u = mx_kscale(H)
    packed_w2 = pack_weight(n((H, N)) / np.sqrt(H) / u[:, None])
    return {
        "xT": (n((K, T)) * s).astype(np.float32),
        "w1": (n((K, H)) / np.sqrt(K) / s).astype(np.float32),
        "w2_words": packed_w2[0],
        "w2_scales": packed_w2[1],
        "gamma": (np.random.uniform(0.5, 1.5, (H, 1)) * u[:, None]).astype(np.float32),
        "offs": striped(np.random.permutation(T)[:S]),
    }


def reference(xT, w1, w2_words, w2_scales, gamma, offs):
    xq = mxq(f64(xT)[:, unstriped(offs)], 0, "e4m3")
    h = mxq(f64(w1), 0, "e4m3").T @ xq
    hn = (h - h.mean(axis=1, keepdims=True)) / np.sqrt(h.var(axis=1, keepdims=True) + 1e-5)
    z = f64(gamma) * hn
    return unpack_weight(w2_words, w2_scales).T @ mxq(z, 0, "e4m3")

@@ -1,0 +1,186 @@
+from contextlib import ExitStack
+
+import concourse.mybir as mybir
+
+K, T, S, H, N = 1024, 1024, 512, 512, 256
+FLOPS = 2 * K * S * H + 2 * H * S * N
+
+F32 = mybir.dt.float32
+BF16 = mybir.dt.bfloat16
+I32 = mybir.dt.int32
+U32 = mybir.dt.uint32
+U16 = mybir.dt.uint16
+U8 = mybir.dt.uint8
+FP8X4 = mybir.dt.float8_e4m3fn_x4
+ACT = mybir.ActivationFunctionType
+ALU = mybir.AluOpType
+
+P = 128
+PACK = 4
+K_PASS = P * PACK
+PASSES = K // K_PASS
+UNIT = 256
+EPS = 1e-5
+
+
+def tile_picked_inorm_none_e_kernel(tc, xT, w1, w2_words, w2_scales, gamma, offs, out):
+    nc = tc.nc
+
+    def cast(on_vector, dst, src):
+        if on_vector:
+            nc.vector.tensor_copy(out=dst, in_=src)
+        else:
+            nc.scalar.activation(out=dst, in_=src, func=ACT.Copy)
+
+    def weave(on_vector, dst, src):
+        cast(on_vector, dst.rearrange("p (c i) t -> p c t i", i=4), src.rearrange("p t (c i) -> p c t i", i=4))
+
+    with ExitStack() as ctx:
+        keep = ctx.enter_context(tc.tile_pool(name="keep", bufs=1))
+        psum = ctx.enter_context(tc.psum_pool(name="psum", bufs=1))
+
+        offsets = keep.tile([P, S // 16], U16, name="offsets")
+        x_scales = keep.tile([P, T], U8, name="x_scales", align_bytes=64)
+        w2_codes = keep.tile([P, N], U32, name="w2_codes", align_bytes=64)
+        w2_plane = keep.tile([P, N], U8, name="w2_plane", align_bytes=64)
+        gam = keep.tile([P, PACK], F32, name="gam")
+        warm = keep.tile([P, 2], F32, name="warm")
+
+        nc.gpsimd.memset(x_scales[:].bitcast(U32), 0)
+        nc.gpsimd.memset(w2_plane[:].bitcast(U32), 0)
+        nc.vector.memset(warm[:, 0:1], 1.0)
+        nc.scalar.activation(out=warm[:, 1:2], in_=warm[:, 0:1], func=ACT.Abs_reciprocal_sqrt)
+
+        x_cuts = [[(0, 512), (512, 1024)], [(0, 512), (512, 768), (768, 1024)]]
+        x_raw = {}
+        for g in range(PASSES):
+            rows = xT[g * K_PASS : (g + 1) * K_PASS, :].rearrange("(p j) n -> p j n", j=PACK)
+            for a, b in x_cuts[g]:
+                raw = keep.tile([P, PACK, b - a], F32, name=f"x_raw_{g}_{a}")
+                nc.sync.dma_start(out=raw[:], in_=rows[:, :, a:b])
+                for u in range(a, b, UNIT):
+                    x_raw[g, u] = raw[:, :, u - a : u - a + UNIT]
+            if g == 0:
+                nc.sync.dma_start(offsets[:], offs)
+        w_raw = {}
+        for g in range(PASSES):
+            rows = w1[g * K_PASS : (g + 1) * K_PASS, :].rearrange("(p j) n -> p j n", j=PACK)
+            for h in range(2):
+                raw = keep.tile([P, PACK, 256], F32, name=f"w_raw_{g}_{h}")
+                nc.sync.dma_start(out=raw[:], in_=rows[:, :, 256 * h : 256 * (h + 1)])
+                w_raw[g, h] = raw
+        nc.sync.dma_start(out=gam[:], in_=gamma.rearrange("(p t) o -> p (t o)", t=PACK))
+        nc.sync.dma_start(out=w2_codes[:].bitcast(I32), in_=w2_words[0].rearrange("p n t -> p (n t)").bitcast(I32))
+        for q in range(4):
+            nc.sync.dma_start(out=w2_plane[32 * q : 32 * q + 4, :].bitcast(I32), in_=w2_scales[0, 4 * q : 4 * q + 4, :].bitcast(I32))
+
+        picked = []
+        for g in range(PASSES):
+            words = keep.tile([P, T], U32, name=f"x_words_{g}", align_bytes=64)
+            for u in range(0, T, UNIT):
+                grouped = keep.tile([P, UNIT, PACK], BF16, name=f"x_grouped_{g}_{u}", align_bytes=64)
+                if g == PASSES - 1 and u == T - UNIT:
+                    weave(False, grouped[:, 0:96, :], x_raw[g, u][:, :, 0:96])
+                    weave(True, grouped[:, 96:UNIT, :], x_raw[g, u][:, :, 96:UNIT])
+                elif g == PASSES - 1 and u == T - 2 * UNIT:
+                    weave(False, grouped[:], x_raw[g, u])
+                else:
+                    weave((u // UNIT) % 2 == 1, grouped[:], x_raw[g, u])
+                nc.vector.quantize_mx(
+                    out=words[:, u : u + UNIT].bitcast(FP8X4),
+                    scales=x_scales[4 * g : P, u : u + UNIT],
+                    in_=grouped[:].rearrange("p n j -> p (n j)"),
+                )
+            got = keep.tile([P, S], U32, name=f"picked_{g}", align_bytes=64)
+            nc.vector.tensor_copy(out=got[:], in_=words[:].indirect(offsets[:]))
+            picked.append(got)
+        picked_scales = keep.tile([P, S], U8, name="picked_scales", align_bytes=64)
+        nc.vector.tensor_copy(out=picked_scales[:], in_=x_scales[:].indirect(offsets[:]))
+
+        w_codes = []
+        w_scales = []
+        for g in range(PASSES):
+            grouped = keep.tile([P, PACK, P, PACK], BF16, name=f"w_grouped_{g}", align_bytes=64)
+            codes = keep.tile([P, H], U32, name=f"w_codes_{g}", align_bytes=64)
+            scales = keep.tile([P, H], U8, name=f"w_scales_{g}", align_bytes=64)
+            for h in range(2):
+                dst = grouped[:, :, 64 * h : 64 * (h + 1), :].rearrange("p t m j -> p m j t")
+                src = w_raw[g, h][:].rearrange("p j (m t) -> p m j t", t=PACK)
+                if g == PASSES - 1 and h == 1:
+                    cast(False, dst[:, 0:22], src[:, 0:22])
+                    cast(True, dst[:, 22:64], src[:, 22:64])
+                else:
+                    cast(False, dst, src)
+            step = P
+            for c in range(0, H, step):
+                nc.vector.quantize_mx(
+                    out=codes[:, c : c + step].bitcast(FP8X4),
+                    scales=scales[:, c : c + step],
+                    in_=grouped[:].rearrange("p t m j -> p (t m j)")[:, PACK * c : PACK * (c + step)],
+                )
+            w_codes.append(codes)
+            w_scales.append(scales)
+
+        banks = [psum.tile([P, S], F32, name=f"h_{t}", tag=f"h_{t}") for t in range(PACK)]
+        for t in range(PACK):
+            for g in range(PASSES):
+                nc.tensor.matmul_mx(
+                    out=banks[t][:],
+                    lhsT=w_codes[g][:, t * P : (t + 1) * P].bitcast(FP8X4),
+                    lhsT_scale=w_scales[g][:, t * P : (t + 1) * P],
+                    rhs=picked[g][:].bitcast(FP8X4),
+                    rhs_scale=picked_scales[4 * g : P, :],
+                    start=(g == 0),
+                    stop=(g == PASSES - 1),
+                )
+
+        z_planes = keep.tile([P, PACK, S], BF16, name="z_planes", align_bytes=64)
+        neg_gam = keep.tile([P, PACK], F32, name="neg_gam")
+        nc.gpsimd.tensor_scalar(out=neg_gam[:], in0=gam[:], scalar1=-1.0, scalar2=0.0, op0=ALU.mult, op1=ALU.add)
+        for t in range(PACK):
+            stats = keep.tile([P, 6], F32, name=f"stats_{t}")
+            moments = keep.tile([P, 2], F32, name=f"moments_{t}")
+            rstd = keep.tile([P, 1], F32, name=f"rstd_{t}")
+            gain = keep.tile([P, 1], F32, name=f"gain_{t}")
+            shift = keep.tile([P, 1], F32, name=f"shift_{t}")
+            nc.vector.bn_stats(out=stats[:], in_=banks[t][:])
+            nc.vector.bn_aggr(out=moments[:], in_=stats[:])
+            nc.scalar.activation(out=rstd[:], in_=moments[:, 1:2], func=ACT.Abs_reciprocal_sqrt, bias=EPS)
+            if t < PACK - 1:
+                nc.gpsimd.tensor_scalar(out=gain[:], in0=rstd[:], scalar1=gam[:, t : t + 1], scalar2=0.0, op0=ALU.mult, op1=ALU.add)
+                nc.gpsimd.tensor_scalar(out=shift[:], in0=rstd[:], scalar1=neg_gam[:, t : t + 1], scalar2=moments[:, 0:1], op0=ALU.mult, op1=ALU.mult)
+                nc.scalar.activation(out=z_planes[:, t, :], in_=banks[t][:], func=ACT.Identity, scale=gain[:], bias=shift[:])
+            else:
+                nc.vector.tensor_scalar(out=gain[:], in0=rstd[:], scalar1=gam[:, t : t + 1], scalar2=None, op0=ALU.mult)
+                nc.vector.tensor_scalar(out=z_planes[:, t, :], in0=banks[t][:], scalar1=moments[:, 0:1], scalar2=gain[:], op0=ALU.subtract, op1=ALU.mult)
+
+        out_rows = out.rearrange("(b p) n -> p b n", p=P)
+        z_grouped = [keep.tile([P, P, PACK], BF16, name=f"z_grouped_{h}", align_bytes=64) for h in range(4)]
+        for h in range(4):
+            weave(h != 2, z_grouped[h][:], z_planes[:, :, h * P : (h + 1) * P])
+        for h in range(4):
+            z_codes = keep.tile([P, P], U32, name=f"z_codes_{h}", align_bytes=64)
+            z_scales = keep.tile([P, P], U8, name=f"z_scales_{h}", align_bytes=64)
+            nc.vector.quantize_mx(out=z_codes[:].bitcast(FP8X4), scales=z_scales[:], in_=z_grouped[h][:].rearrange("p n j -> p (n j)"))
+            result = keep.tile([P, 2, P], F32, name=f"result_{h}")
+            if h < 3:
+                both = psum.tile([P, 2, P], F32, name=f"acc_{h}", tag=f"h_{h}")
+                accs = [both[:, 0, :], both[:, 1, :]]
+            else:
+                accs = [psum.tile([P, P], F32, name=f"acc_last_{b}")[:] for b in range(2)]
+            for b in range(2):
+                nc.tensor.matmul_mx(
+                    out=accs[b],
+                    lhsT=w2_codes[:, b * P : (b + 1) * P].bitcast(FP8X4),
+                    lhsT_scale=w2_plane[:, b * P : (b + 1) * P],
+                    rhs=z_codes[:].bitcast(FP8X4),
+                    rhs_scale=z_scales[:],
+                    start=True,
+                    stop=True,
+                )
+            if h < 3:
+                cast(False, result[:], both[:])
+            else:
+                for b in range(2):
+                    cast(b == 1, result[:, b, :], accs[b])
+            nc.sync.dma_start(out=out_rows[:, :, h * P : (h + 1) * P], in_=result[:])

@@ -80,8 +80,8 @@ def tile_picked_inorm_none_e_kernel(tc, xT, w1, w2_words, w2_scales, gamma, offs
             for u in range(0, T, UNIT):
                 grouped = keep.tile([P, UNIT, PACK], BF16, name=f"x_grouped_{g}_{u}", align_bytes=64)
                 if g == PASSES - 1 and u == T - UNIT:
-                    weave(False, grouped[:, 0:96, :], x_raw[g, u][:, :, 0:96])
-                    weave(True, grouped[:, 96:UNIT, :], x_raw[g, u][:, :, 96:UNIT])
+                    weave(False, grouped[:, 0:64, :], x_raw[g, u][:, :, 0:64])
+                    weave(True, grouped[:, 64:UNIT, :], x_raw[g, u][:, :, 64:UNIT])
                 elif g == PASSES - 1 and u == T - 2 * UNIT:
                     weave(False, grouped[:], x_raw[g, u])
                 else:
@@ -107,8 +107,8 @@ def tile_picked_inorm_none_e_kernel(tc, xT, w1, w2_words, w2_scales, gamma, offs
                 dst = grouped[:, :, 64 * h : 64 * (h + 1), :].rearrange("p t m j -> p m j t")
                 src = w_raw[g, h][:].rearrange("p j (m t) -> p m j t", t=PACK)
                 if g == PASSES - 1 and h == 1:
-                    cast(False, dst[:, 0:22], src[:, 0:22])
-                    cast(True, dst[:, 22:64], src[:, 22:64])
+                    cast(False, dst[:, 0:16], src[:, 0:16])
+                    cast(True, dst[:, 16:64], src[:, 16:64])
                 else:
                     cast(False, dst, src)
             step = P
@@ -135,29 +135,49 @@ def tile_picked_inorm_none_e_kernel(tc, xT, w1, w2_words, w2_scales, gamma, offs
                 )
 
         z_planes = keep.tile([P, PACK, S], BF16, name="z_planes", align_bytes=64)
-        neg_gam = keep.tile([P, PACK], F32, name="neg_gam")
-        nc.gpsimd.tensor_scalar(out=neg_gam[:], in0=gam[:], scalar1=-1.0, scalar2=0.0, op0=ALU.mult, op1=ALU.add)
-        for t in range(PACK):
-            stats = keep.tile([P, 6], F32, name=f"stats_{t}")
-            moments = keep.tile([P, 2], F32, name=f"moments_{t}")
-            rstd = keep.tile([P, 1], F32, name=f"rstd_{t}")
-            gain = keep.tile([P, 1], F32, name=f"gain_{t}")
-            shift = keep.tile([P, 1], F32, name=f"shift_{t}")
-            nc.vector.bn_stats(out=stats[:], in_=banks[t][:])
-            nc.vector.bn_aggr(out=moments[:], in_=stats[:])
-            nc.scalar.activation(out=rstd[:], in_=moments[:, 1:2], func=ACT.Abs_reciprocal_sqrt, bias=EPS)
-            if t < PACK - 1:
-                nc.gpsimd.tensor_scalar(out=gain[:], in0=rstd[:], scalar1=gam[:, t : t + 1], scalar2=0.0, op0=ALU.mult, op1=ALU.add)
-                nc.gpsimd.tensor_scalar(out=shift[:], in0=rstd[:], scalar1=neg_gam[:, t : t + 1], scalar2=moments[:, 0:1], op0=ALU.mult, op1=ALU.mult)
-                nc.scalar.activation(out=z_planes[:, t, :], in_=banks[t][:], func=ACT.Identity, scale=gain[:], bias=shift[:])
-            else:
-                nc.vector.tensor_scalar(out=gain[:], in0=rstd[:], scalar1=gam[:, t : t + 1], scalar2=None, op0=ALU.mult)
-                nc.vector.tensor_scalar(out=z_planes[:, t, :], in0=banks[t][:], scalar1=moments[:, 0:1], scalar2=gain[:], op0=ALU.subtract, op1=ALU.mult)
+        last = PACK - 1
+        stats = [keep.tile([P, 6], F32, name=f"stats_{t}") for t in range(PACK)]
+        moments = [keep.tile([P, 2, 2], F32, name=f"moments_{u}") for u in range(2)]
+        rstd = [keep.tile([P, 2], F32, name=f"rstd_{u}") for u in range(2)]
+        gain = [keep.tile([P, 2], F32, name=f"gain_{u}") for u in range(2)]
+        h_copy = [keep.tile([P, S], F32, name=f"h_copy_{t}") for t in range(last)]
+        neg_gam = keep.tile([P, 1], F32, name="neg_gam")
+        factors = keep.tile([P, 2], F32, name="factors")
+        affine = keep.tile([P, 2], F32, name="affine")
+        nc.scalar.activation(out=neg_gam[:], in_=gam[:, last:PACK], func=ACT.Identity, scale=-1.0)
+        nc.scalar.activation(out=factors[:, 0:1], in_=gam[:, last:PACK], func=ACT.Identity)
 
+        def aggregate(t):
+            nc.vector.bn_aggr(out=moments[t // 2][:, t % 2, :], in_=stats[t][:])
+
+        def inverse_root(u):
+            nc.scalar.activation(out=rstd[u][:], in_=moments[u][:, :, 1], func=ACT.Abs_reciprocal_sqrt, bias=EPS)
+
+        def normalise(t):
+            nc.vector.tensor_scalar(out=z_planes[:, t, :], in0=h_copy[t][:], scalar1=moments[t // 2][:, t % 2, 0:1], scalar2=gain[t // 2][:, t % 2 : t % 2 + 1], op0=ALU.subtract, op1=ALU.mult)
+
+        for t in range(PACK):
+            nc.vector.bn_stats(out=stats[t][:], in_=banks[t][:])
+            if t > 0:
+                aggregate(t - 1)
+            if t == 2:
+                inverse_root(0)
+            if t < last:
+                nc.scalar.activation(out=h_copy[t][:], in_=banks[t][:], func=ACT.Copy)
+        nc.vector.tensor_tensor(out=gain[0][:], in0=rstd[0][:], in1=gam[:, 0:2], op=ALU.mult)
+        aggregate(last)
+        inverse_root(1)
+        nc.scalar.activation(out=factors[:, 1:2], in_=moments[1][:, 1, 0:1], func=ACT.Identity, scale=neg_gam[:])
+        nc.scalar.activation(out=gain[1][:, 0:1], in_=rstd[1][:, 0:1], func=ACT.Identity, scale=gam[:, 2:3])
+        nc.scalar.activation(out=affine[:], in_=factors[:], func=ACT.Identity, scale=rstd[1][:, 1:2])
+        nc.scalar.activation(out=z_planes[:, last, :], in_=banks[last][:], func=ACT.Identity, scale=affine[:, 0:1], bias=affine[:, 1:2])
+        normalise(0)
+        normalise(1)
+        normalise(2)
         out_rows = out.rearrange("(b p) n -> p b n", p=P)
         z_grouped = [keep.tile([P, P, PACK], BF16, name=f"z_grouped_{h}", align_bytes=64) for h in range(4)]
         for h in range(4):
-            weave(h != 2, z_grouped[h][:], z_planes[:, :, h * P : (h + 1) * P])
+            weave(h < 2, z_grouped[h][:], z_planes[:, :, h * P : (h + 1) * P])
         for h in range(4):
             z_codes = keep.tile([P, P], U32, name=f"z_codes_{h}", align_bytes=64)
             z_scales = keep.tile([P, P], U8, name=f"z_scales_{h}", align_bytes=64)
@@ -179,7 +199,7 @@ def tile_picked_inorm_none_e_kernel(tc, xT, w1, w2_words, w2_scales, gamma, offs
                     stop=True,
                 )
             if h < 3:
-                cast(False, result[:], both[:])
+                cast(h == 1, result[:], both[:])
             else:
                 for b in range(2):
                     cast(b == 1, result[:, b, :], accs[b])

@@ -63,12 +63,13 @@ def tile_picked_inorm_none_e_kernel(tc, xT, w1, w2_words, w2_scales, gamma, offs
             if g == 0:
                 nc.sync.dma_start(offsets[:], offs)
         w_raw = {}
+        w_cuts = [[(0, 64, 64), (64, 128, 64)], [(0, 64, 64), (64, 96, 0), (96, 128, 8)]]
         for g in range(PASSES):
             rows = w1[g * K_PASS : (g + 1) * K_PASS, :].rearrange("(p j) n -> p j n", j=PACK)
-            for h in range(2):
-                raw = keep.tile([P, PACK, 256], F32, name=f"w_raw_{g}_{h}")
-                nc.sync.dma_start(out=raw[:], in_=rows[:, :, 256 * h : 256 * (h + 1)])
-                w_raw[g, h] = raw
+            for a, b, s in w_cuts[g]:
+                raw = keep.tile([P, PACK, PACK * (b - a)], F32, name=f"w_raw_{g}_{a}")
+                nc.sync.dma_start(out=raw[:], in_=rows[:, :, PACK * a : PACK * b])
+                w_raw[g, a] = raw
         nc.sync.dma_start(out=gam[:], in_=gamma.rearrange("(p t) o -> p (t o)", t=PACK))
         nc.sync.dma_start(out=w2_codes[:].bitcast(I32), in_=w2_words[0].rearrange("p n t -> p (n t)").bitcast(I32))
         for q in range(4):
@@ -97,55 +98,54 @@ def tile_picked_inorm_none_e_kernel(tc, xT, w1, w2_words, w2_scales, gamma, offs
         picked_scales = keep.tile([P, S], U8, name="picked_scales", align_bytes=64)
         nc.vector.tensor_copy(out=picked_scales[:], in_=x_scales[:].indirect(offsets[:]))
 
-        w_codes = []
-        w_scales = []
+        w_grouped = []
         for g in range(PASSES):
             grouped = keep.tile([P, PACK, P, PACK], BF16, name=f"w_grouped_{g}", align_bytes=64)
-            codes = keep.tile([P, H], U32, name=f"w_codes_{g}", align_bytes=64)
-            scales = keep.tile([P, H], U8, name=f"w_scales_{g}", align_bytes=64)
-            for h in range(2):
-                dst = grouped[:, :, 64 * h : 64 * (h + 1), :].rearrange("p t m j -> p m j t")
-                src = w_raw[g, h][:].rearrange("p j (m t) -> p m j t", t=PACK)
-                if g == PASSES - 1 and h == 1:
-                    cast(False, dst[:, 0:16], src[:, 0:16])
-                    cast(True, dst[:, 16:64], src[:, 16:64])
-                else:
-                    cast(False, dst, src)
-            step = P
-            for c in range(0, H, step):
-                nc.vector.quantize_mx(
-                    out=codes[:, c : c + step].bitcast(FP8X4),
-                    scales=scales[:, c : c + step],
-                    in_=grouped[:].rearrange("p t m j -> p (t m j)")[:, PACK * c : PACK * (c + step)],
-                )
-            w_codes.append(codes)
-            w_scales.append(scales)
+            for a, b, s in w_cuts[g]:
+                dst = grouped[:, :, a:b, :].rearrange("p t m j -> p m j t")
+                src = w_raw[g, a][:].rearrange("p j (m t) -> p m j t", t=PACK)
+                if s > 0:
+                    cast(False, dst[:, 0:s], src[:, 0:s])
+                if s < b - a:
+                    cast(True, dst[:, s : b - a], src[:, s : b - a])
+            w_grouped.append(grouped)
+        w_codes = {}
+        w_scales = {}
+        for g, t in [(0, 0), (0, 1), (1, 0), (1, 1), (0, 2), (1, 2), (0, 3), (1, 3)]:
+            codes = keep.tile([P, P], U32, name=f"w_codes_{g}_{t}", align_bytes=64)
+            if g == 0 and t >= 2:
+                w_scales[g, t] = plane[4:P, :]
+            else:
+                plane = keep.tile([P, P], U8, name=f"w_scales_{g}_{t}", align_bytes=64)
+                w_scales[g, t] = plane[:]
+            nc.vector.quantize_mx(
+                out=codes[:].bitcast(FP8X4),
+                scales=w_scales[g, t],
+                in_=w_grouped[g][:, t].rearrange("p m j -> p (m j)"),
+            )
+            w_codes[g, t] = codes
 
-        banks = [psum.tile([P, S], F32, name=f"h_{t}", tag=f"h_{t}") for t in range(PACK)]
-        for t in range(PACK):
-            for g in range(PASSES):
+        pieces = {t: [(0, S)] if t < PACK - 1 else [(0, S // 2), (S // 2, S)] for t in range(PACK)}
+        banks = {(t, a): psum.tile([P, b - a], F32, name=f"h_{t}_{a}", tag=f"h_{t}_{a}") for t in range(PACK) for a, b in pieces[t]}
+        for g, t in [(0, 0), (0, 1), (1, 0), (1, 1), (0, 2), (1, 2), (0, 3), (1, 3)]:
+            for a, b in pieces[t]:
                 nc.tensor.matmul_mx(
-                    out=banks[t][:],
-                    lhsT=w_codes[g][:, t * P : (t + 1) * P].bitcast(FP8X4),
-                    lhsT_scale=w_scales[g][:, t * P : (t + 1) * P],
-                    rhs=picked[g][:].bitcast(FP8X4),
-                    rhs_scale=picked_scales[4 * g : P, :],
+                    out=banks[t, a][:],
+                    lhsT=w_codes[g, t][:].bitcast(FP8X4),
+                    lhsT_scale=w_scales[g, t],
+                    rhs=picked[g][:, a:b].bitcast(FP8X4),
+                    rhs_scale=picked_scales[4 * g : P, a:b],
                     start=(g == 0),
                     stop=(g == PASSES - 1),
                 )
 
         z_planes = keep.tile([P, PACK, S], BF16, name="z_planes", align_bytes=64)
-        last = PACK - 1
-        stats = [keep.tile([P, 6], F32, name=f"stats_{t}") for t in range(PACK)]
+        stats = [keep.tile([P, 6 * len(pieces[t])], F32, name=f"stats_{t}") for t in range(PACK)]
         moments = [keep.tile([P, 2, 2], F32, name=f"moments_{u}") for u in range(2)]
         rstd = [keep.tile([P, 2], F32, name=f"rstd_{u}") for u in range(2)]
         gain = [keep.tile([P, 2], F32, name=f"gain_{u}") for u in range(2)]
-        h_copy = [keep.tile([P, S], F32, name=f"h_copy_{t}") for t in range(last)]
-        neg_gam = keep.tile([P, 1], F32, name="neg_gam")
-        factors = keep.tile([P, 2], F32, name="factors")
-        affine = keep.tile([P, 2], F32, name="affine")
-        nc.scalar.activation(out=neg_gam[:], in_=gam[:, last:PACK], func=ACT.Identity, scale=-1.0)
-        nc.scalar.activation(out=factors[:, 0:1], in_=gam[:, last:PACK], func=ACT.Identity)
+        h_copy = [keep.tile([P, S], F32, name=f"h_copy_{t}") for t in range(PACK)]
+        z_grouped = [keep.tile([P, P, PACK], BF16, name=f"z_grouped_{h}", align_bytes=64) for h in range(4)]
 
         def aggregate(t):
             nc.vector.bn_aggr(out=moments[t // 2][:, t % 2, :], in_=stats[t][:])
@@ -153,38 +153,44 @@ def tile_picked_inorm_none_e_kernel(tc, xT, w1, w2_words, w2_scales, gamma, offs
         def inverse_root(u):
             nc.scalar.activation(out=rstd[u][:], in_=moments[u][:, :, 1], func=ACT.Abs_reciprocal_sqrt, bias=EPS)
 
-        def normalise(t):
-            nc.vector.tensor_scalar(out=z_planes[:, t, :], in0=h_copy[t][:], scalar1=moments[t // 2][:, t % 2, 0:1], scalar2=gain[t // 2][:, t % 2 : t % 2 + 1], op0=ALU.subtract, op1=ALU.mult)
+        def normalise(t, a, b):
+            nc.vector.tensor_scalar(out=z_planes[:, t, a:b], in0=h_copy[t][:, a:b], scalar1=moments[t // 2][:, t % 2, 0:1], scalar2=gain[t // 2][:, t % 2 : t % 2 + 1], op0=ALU.subtract, op1=ALU.mult)
+
+        def weave_z(on_vector, h):
+            weave(on_vector, z_grouped[h][:], z_planes[:, :, h * P : (h + 1) * P])
 
         for t in range(PACK):
-            nc.vector.bn_stats(out=stats[t][:], in_=banks[t][:])
-            if t > 0:
-                aggregate(t - 1)
-            if t == 2:
-                inverse_root(0)
-            if t < last:
-                nc.scalar.activation(out=h_copy[t][:], in_=banks[t][:], func=ACT.Copy)
+            for n, (a, b) in enumerate(pieces[t]):
+                nc.vector.bn_stats(out=stats[t][:, 6 * n : 6 * n + 6], in_=banks[t, a][:])
+                if t > 0 and n == 0:
+                    aggregate(t - 1)
+                if t == 2:
+                    inverse_root(0)
+                nc.scalar.activation(out=h_copy[t][:, a:b], in_=banks[t, a][:], func=ACT.Copy)
         nc.vector.tensor_tensor(out=gain[0][:], in0=rstd[0][:], in1=gam[:, 0:2], op=ALU.mult)
-        aggregate(last)
+        aggregate(3)
         inverse_root(1)
-        nc.scalar.activation(out=factors[:, 1:2], in_=moments[1][:, 1, 0:1], func=ACT.Identity, scale=neg_gam[:])
-        nc.scalar.activation(out=gain[1][:, 0:1], in_=rstd[1][:, 0:1], func=ACT.Identity, scale=gam[:, 2:3])
-        nc.scalar.activation(out=affine[:], in_=factors[:], func=ACT.Identity, scale=rstd[1][:, 1:2])
-        nc.scalar.activation(out=z_planes[:, last, :], in_=banks[last][:], func=ACT.Identity, scale=affine[:, 0:1], bias=affine[:, 1:2])
-        normalise(0)
-        normalise(1)
-        normalise(2)
+        normalise(0, 0, S)
+        normalise(1, 0, S)
+        for t in (2, 3):
+            nc.scalar.activation(out=gain[1][:, t - 2 : t - 1], in_=rstd[1][:, t - 2 : t - 1], func=ACT.Identity, scale=gam[:, t : t + 1])
+        normalise(2, 0, 256)
+        normalise(3, 0, 256)
+        normalise(2, 256, S)
+        weave_z(False, 1)
+        weave_z(True, 0)
+        normalise(3, 256, S)
+        weave_z(False, 3)
         out_rows = out.rearrange("(b p) n -> p b n", p=P)
-        z_grouped = [keep.tile([P, P, PACK], BF16, name=f"z_grouped_{h}", align_bytes=64) for h in range(4)]
         for h in range(4):
-            weave(h < 2, z_grouped[h][:], z_planes[:, :, h * P : (h + 1) * P])
-        for h in range(4):
+            if h == 1:
+                weave_z(True, 2)
             z_codes = keep.tile([P, P], U32, name=f"z_codes_{h}", align_bytes=64)
             z_scales = keep.tile([P, P], U8, name=f"z_scales_{h}", align_bytes=64)
             nc.vector.quantize_mx(out=z_codes[:].bitcast(FP8X4), scales=z_scales[:], in_=z_grouped[h][:].rearrange("p n j -> p (n j)"))
             result = keep.tile([P, 2, P], F32, name=f"result_{h}")
             if h < 3:
-                both = psum.tile([P, 2, P], F32, name=f"acc_{h}", tag=f"h_{h}")
+                both = psum.tile([P, 2, P], F32, name=f"acc_{h}", tag=f"h_{h}_0")
                 accs = [both[:, 0, :], both[:, 1, :]]
             else:
                 accs = [psum.tile([P, P], F32, name=f"acc_last_{b}")[:] for b in range(2)]

@@ -46,8 +46,8 @@ def tile_picked_inorm_none_e_kernel(tc, xT, w1, w2_words, w2_scales, gamma, offs
         gam = keep.tile([P, PACK], F32, name="gam")
         warm = keep.tile([P, 2], F32, name="warm")
 
-        nc.gpsimd.memset(x_scales[:].bitcast(U32), 0)
-        nc.gpsimd.memset(w2_plane[:].bitcast(U32), 0)
+        nc.vector.memset(x_scales[:].bitcast(U32), 0)
+        nc.vector.memset(w2_plane[:].bitcast(U32), 0)
         nc.vector.memset(warm[:, 0:1], 1.0)
         nc.scalar.activation(out=warm[:, 1:2], in_=warm[:, 0:1], func=ACT.Abs_reciprocal_sqrt)
 
@@ -125,7 +125,7 @@ def tile_picked_inorm_none_e_kernel(tc, xT, w1, w2_words, w2_scales, gamma, offs
             )
             w_codes[g, t] = codes
 
-        pieces = {t: [(0, S)] if t < PACK - 1 else [(0, S // 2), (S // 2, S)] for t in range(PACK)}
+        pieces = {t: [(0, S)] if t in (1, 2) else [(0, S // 2), (S // 2, S)] for t in range(PACK)}
         banks = {(t, a): psum.tile([P, b - a], F32, name=f"h_{t}_{a}", tag=f"h_{t}_{a}") for t in range(PACK) for a, b in pieces[t]}
         for g, t in [(0, 0), (0, 1), (1, 0), (1, 1), (0, 2), (1, 2), (0, 3), (1, 3)]:
             for a, b in pieces[t]:
@@ -141,59 +141,84 @@ def tile_picked_inorm_none_e_kernel(tc, xT, w1, w2_words, w2_scales, gamma, offs
 
         z_planes = keep.tile([P, PACK, S], BF16, name="z_planes", align_bytes=64)
         stats = [keep.tile([P, 6 * len(pieces[t])], F32, name=f"stats_{t}") for t in range(PACK)]
-        moments = [keep.tile([P, 2, 2], F32, name=f"moments_{u}") for u in range(2)]
-        rstd = [keep.tile([P, 2], F32, name=f"rstd_{u}") for u in range(2)]
-        gain = [keep.tile([P, 2], F32, name=f"gain_{u}") for u in range(2)]
+        moments = keep.tile([P, PACK, 2], F32, name="moments")
+        rstd = keep.tile([P, PACK], F32, name="rstd")
+        shift = keep.tile([P, PACK], F32, name="shift")
         h_copy = [keep.tile([P, S], F32, name=f"h_copy_{t}") for t in range(PACK)]
         z_grouped = [keep.tile([P, P, PACK], BF16, name=f"z_grouped_{h}", align_bytes=64) for h in range(4)]
 
-        def aggregate(t):
-            nc.vector.bn_aggr(out=moments[t // 2][:, t % 2, :], in_=stats[t][:])
+        def statistics(t, n):
+            a, b = pieces[t][n]
+            nc.vector.bn_stats(out=stats[t][:, 6 * n : 6 * n + 6], in_=banks[t, a][:])
 
-        def inverse_root(u):
-            nc.scalar.activation(out=rstd[u][:], in_=moments[u][:, :, 1], func=ACT.Abs_reciprocal_sqrt, bias=EPS)
+        def copy_out(t, n):
+            a, b = pieces[t][n]
+            nc.scalar.activation(out=h_copy[t][:, a:b], in_=banks[t, a][:], func=ACT.Copy, scale=gam[:, t : t + 1])
+
+        def aggregate(t):
+            nc.vector.bn_aggr(out=moments[:, t, :], in_=stats[t][:])
+
+        def inverse_root(t0, t1):
+            nc.scalar.activation(out=rstd[:, t0:t1], in_=moments[:, t0:t1, 1], func=ACT.Abs_reciprocal_sqrt, bias=EPS)
+
+        def scaled_mean(t0, t1):
+            nc.vector.tensor_tensor(out=shift[:, t0:t1], in0=moments[:, t0:t1, 0], in1=gam[:, t0:t1], op=ALU.mult)
 
         def normalise(t, a, b):
-            nc.vector.tensor_scalar(out=z_planes[:, t, a:b], in0=h_copy[t][:, a:b], scalar1=moments[t // 2][:, t % 2, 0:1], scalar2=gain[t // 2][:, t % 2 : t % 2 + 1], op0=ALU.subtract, op1=ALU.mult)
+            nc.vector.tensor_scalar(out=z_planes[:, t, a:b], in0=h_copy[t][:, a:b], scalar1=shift[:, t : t + 1], scalar2=rstd[:, t : t + 1], op0=ALU.subtract, op1=ALU.mult)
 
-        def weave_z(on_vector, h):
-            weave(on_vector, z_grouped[h][:], z_planes[:, :, h * P : (h + 1) * P])
+        def weave_z(on_vector, h, a=0, b=P):
+            dst = z_grouped[h][:, a:b, :].rearrange("p (c i) t -> p c t i", i=4)
+            src = z_planes[:, :, h * P + a : h * P + b].rearrange("p t (c i) -> p c t i", i=4)
+            if on_vector:
+                nc.vector.tensor_copy(out=dst, in_=src)
+            else:
+                nc.scalar.copy(out=dst, in_=src)
 
-        for t in range(PACK):
-            for n, (a, b) in enumerate(pieces[t]):
-                nc.vector.bn_stats(out=stats[t][:, 6 * n : 6 * n + 6], in_=banks[t, a][:])
-                if t > 0 and n == 0:
-                    aggregate(t - 1)
-                if t == 2:
-                    inverse_root(0)
-                nc.scalar.activation(out=h_copy[t][:, a:b], in_=banks[t, a][:], func=ACT.Copy)
-        nc.vector.tensor_tensor(out=gain[0][:], in0=rstd[0][:], in1=gam[:, 0:2], op=ALU.mult)
-        aggregate(3)
-        inverse_root(1)
+        statistics(0, 0)
+        copy_out(0, 0)
+        statistics(0, 1)
+        copy_out(0, 1)
+        statistics(1, 0)
+        aggregate(0)
+        copy_out(1, 0)
+        inverse_root(0, 1)
+        statistics(2, 0)
+        aggregate(1)
+        scaled_mean(0, 1)
+        copy_out(2, 0)
+        statistics(3, 0)
+        aggregate(2)
+        inverse_root(1, 3)
+        copy_out(3, 0)
+        statistics(3, 1)
+        scaled_mean(1, 3)
         normalise(0, 0, S)
+        aggregate(3)
+        inverse_root(3, 4)
+        copy_out(3, 1)
         normalise(1, 0, S)
-        for t in (2, 3):
-            nc.scalar.activation(out=gain[1][:, t - 2 : t - 1], in_=rstd[1][:, t - 2 : t - 1], func=ACT.Identity, scale=gam[:, t : t + 1])
-        normalise(2, 0, 256)
+        scaled_mean(3, 4)
+        normalise(2, 0, S)
         normalise(3, 0, 256)
-        normalise(2, 256, S)
         weave_z(False, 1)
-        weave_z(True, 0)
         normalise(3, 256, S)
-        weave_z(False, 3)
+        weave_z(True, 0)
+        weave_z(False, 3, 0, 64)
+        weave_z(True, 2)
+        weave_z(True, 3, 64, P)
+        acc_tags = {1: ("h_0_0", "h_0_256"), 2: ("h_2_0", "h_3_0"), 3: ("spare_0", "spare_1")}
         out_rows = out.rearrange("(b p) n -> p b n", p=P)
         for h in range(4):
-            if h == 1:
-                weave_z(True, 2)
             z_codes = keep.tile([P, P], U32, name=f"z_codes_{h}", align_bytes=64)
             z_scales = keep.tile([P, P], U8, name=f"z_scales_{h}", align_bytes=64)
             nc.vector.quantize_mx(out=z_codes[:].bitcast(FP8X4), scales=z_scales[:], in_=z_grouped[h][:].rearrange("p n j -> p (n j)"))
             result = keep.tile([P, 2, P], F32, name=f"result_{h}")
-            if h < 3:
-                both = psum.tile([P, 2, P], F32, name=f"acc_{h}", tag=f"h_{h}_0")
+            if h == 0:
+                both = psum.tile([P, 2, P], F32, name="acc_0", tag="h_1_0")
                 accs = [both[:, 0, :], both[:, 1, :]]
             else:
-                accs = [psum.tile([P, P], F32, name=f"acc_last_{b}")[:] for b in range(2)]
+                accs = [psum.tile([P, P], F32, name=f"acc_{h}_{b}", tag=acc_tags[h][b])[:] for b in range(2)]
             for b in range(2):
                 nc.tensor.matmul_mx(
                     out=accs[b],
@@ -204,8 +229,8 @@ def tile_picked_inorm_none_e_kernel(tc, xT, w1, w2_words, w2_scales, gamma, offs
                     start=True,
                     stop=True,
                 )
-            if h < 3:
-                cast(h == 1, result[:], both[:])
+            if h == 0:
+                cast(False, result[:], both[:])
             else:
                 for b in range(2):
                     cast(b == 1, result[:, b, :], accs[b])

@@ -19,7 +19,6 @@ P = 128
 PACK = 4
 K_PASS = P * PACK
 PASSES = K // K_PASS
-UNIT = 256
 EPS = 1e-5
 
 
@@ -40,75 +39,63 @@ def tile_picked_inorm_none_e_kernel(tc, xT, w1, w2_words, w2_scales, gamma, offs
         psum = ctx.enter_context(tc.psum_pool(name="psum", bufs=1))
 
         offsets = keep.tile([P, S // 16], U16, name="offsets")
-        x_scales = keep.tile([P, T], U8, name="x_scales", align_bytes=64)
         w2_codes = keep.tile([P, N], U32, name="w2_codes", align_bytes=64)
         w2_plane = keep.tile([P, N], U8, name="w2_plane", align_bytes=64)
         gam = keep.tile([P, PACK], F32, name="gam")
         warm = keep.tile([P, 2], F32, name="warm")
 
-        nc.vector.memset(x_scales[:].bitcast(U32), 0)
         nc.vector.memset(w2_plane[:].bitcast(U32), 0)
         nc.vector.memset(warm[:, 0:1], 1.0)
         nc.scalar.activation(out=warm[:, 1:2], in_=warm[:, 0:1], func=ACT.Abs_reciprocal_sqrt)
 
-        x_cuts = [[(0, 512), (512, 1024)], [(0, 512), (512, 768), (768, 1024)]]
         x_raw = {}
         for g in range(PASSES):
             rows = xT[g * K_PASS : (g + 1) * K_PASS, :].rearrange("(p j) n -> p j n", j=PACK)
-            for a, b in x_cuts[g]:
-                raw = keep.tile([P, PACK, b - a], F32, name=f"x_raw_{g}_{a}")
-                nc.sync.dma_start(out=raw[:], in_=rows[:, :, a:b])
-                for u in range(a, b, UNIT):
-                    x_raw[g, u] = raw[:, :, u - a : u - a + UNIT]
-            if g == 0:
-                nc.sync.dma_start(offsets[:], offs)
-        w_raw = {}
-        w_cuts = [[(0, 64, 64), (64, 128, 64)], [(0, 64, 64), (64, 96, 0), (96, 128, 8)]]
+            for u in range(2):
+                x_raw[g, u] = keep.tile([P, 2, T], F32, name=f"x_raw_{g}_{u}")
+                nc.sync.dma_start(out=x_raw[g, u][:], in_=rows[:, 2 * u : 2 * u + 2, :])
+                if (g, u) == (0, 0):
+                    nc.sync.dma_start(offsets[:], offs)
+
+        w_raw = []
         for g in range(PASSES):
-            rows = w1[g * K_PASS : (g + 1) * K_PASS, :].rearrange("(p j) n -> p j n", j=PACK)
-            for a, b, s in w_cuts[g]:
-                raw = keep.tile([P, PACK, PACK * (b - a)], F32, name=f"w_raw_{g}_{a}")
-                nc.sync.dma_start(out=raw[:], in_=rows[:, :, PACK * a : PACK * b])
-                w_raw[g, a] = raw
+            raw = keep.tile([P, PACK, H], F32, name=f"w_raw_{g}")
+            nc.sync.dma_start(out=raw[:], in_=w1[g * K_PASS : (g + 1) * K_PASS, :].rearrange("(p j) n -> p j n", j=PACK))
+            w_raw.append(raw)
         nc.sync.dma_start(out=gam[:], in_=gamma.rearrange("(p t) o -> p (t o)", t=PACK))
         nc.sync.dma_start(out=w2_codes[:].bitcast(I32), in_=w2_words[0].rearrange("p n t -> p (n t)").bitcast(I32))
         for q in range(4):
             nc.sync.dma_start(out=w2_plane[32 * q : 32 * q + 4, :].bitcast(I32), in_=w2_scales[0, 4 * q : 4 * q + 4, :].bitcast(I32))
 
         picked = []
+        picked_scales = []
+        x_on_vector = [[688,544],[208,224]]
         for g in range(PASSES):
-            words = keep.tile([P, T], U32, name=f"x_words_{g}", align_bytes=64)
-            for u in range(0, T, UNIT):
-                grouped = keep.tile([P, UNIT, PACK], BF16, name=f"x_grouped_{g}_{u}", align_bytes=64)
-                if g == PASSES - 1 and u == T - UNIT:
-                    weave(False, grouped[:, 0:64, :], x_raw[g, u][:, :, 0:64])
-                    weave(True, grouped[:, 64:UNIT, :], x_raw[g, u][:, :, 64:UNIT])
-                elif g == PASSES - 1 and u == T - 2 * UNIT:
-                    weave(False, grouped[:], x_raw[g, u])
-                else:
-                    weave((u // UNIT) % 2 == 1, grouped[:], x_raw[g, u])
-                nc.vector.quantize_mx(
-                    out=words[:, u : u + UNIT].bitcast(FP8X4),
-                    scales=x_scales[4 * g : P, u : u + UNIT],
-                    in_=grouped[:].rearrange("p n j -> p (n j)"),
-                )
-            got = keep.tile([P, S], U32, name=f"picked_{g}", align_bytes=64)
-            nc.vector.tensor_copy(out=got[:], in_=words[:].indirect(offsets[:]))
-            picked.append(got)
-        picked_scales = keep.tile([P, S], U8, name="picked_scales", align_bytes=64)
-        nc.vector.tensor_copy(out=picked_scales[:], in_=x_scales[:].indirect(offsets[:]))
+            grouped = keep.tile([P, S, PACK], BF16, name=f"x_grouped_{g}", align_bytes=64)
+            grouped_words = grouped[:].rearrange("p n j -> p (n j)").bitcast(U32).rearrange("p (n u) -> p n u", u=2)
+            for u in range(2):
+                cut = x_on_vector[g][u]
+                pairs = keep.tile([P, T], U32, name=f"x_pairs_{g}_{u}", align_bytes=64)
+                halves = pairs[:].bitcast(BF16).rearrange("p (n j) -> p n j", j=2)
+                weave(False, halves[:, cut:T, :], x_raw[g, u][:, :, cut:T])
+                weave(True, halves[:, 0:cut, :], x_raw[g, u][:, :, 0:cut])
+                nc.vector.tensor_copy(out=grouped_words[:, :, u], in_=pairs[:].indirect(offsets[:]))
+            codes = keep.tile([P, S], U32, name=f"picked_{g}", align_bytes=64)
+            scales = keep.tile([P, S], U8, name=f"picked_scales_{g}", align_bytes=64)
+            nc.vector.quantize_mx(out=codes[:].bitcast(FP8X4), scales=scales[:], in_=grouped[:].rearrange("p n j -> p (n j)"))
+            picked.append(codes)
+            picked_scales.append(scales)
 
-        w_grouped = []
+        w_grouped = {}
         for g in range(PASSES):
-            grouped = keep.tile([P, PACK, P, PACK], BF16, name=f"w_grouped_{g}", align_bytes=64)
-            for a, b, s in w_cuts[g]:
-                dst = grouped[:, :, a:b, :].rearrange("p t m j -> p m j t")
-                src = w_raw[g, a][:].rearrange("p j (m t) -> p m j t", t=PACK)
-                if s > 0:
-                    cast(False, dst[:, 0:s], src[:, 0:s])
-                if s < b - a:
-                    cast(True, dst[:, s : b - a], src[:, s : b - a])
-            w_grouped.append(grouped)
+            for u in range(2):
+                w_grouped[g, u] = keep.tile([P, 2, P, PACK], BF16, name=f"w_grouped_{g}_{u}", align_bytes=64)
+                dst = w_grouped[g, u][:].rearrange("p t m j -> p m j t")
+                src = w_raw[g][:].rearrange("p j (m t) -> p m j t", t=PACK)[:, :, :, 2 * u : 2 * u + 2]
+                cut = [[128,128],[60,88]][g][u]
+                cast(False, dst[:, 0:cut], src[:, 0:cut])
+                if cut < P:
+                    cast(True, dst[:, cut:P], src[:, cut:P])
         w_codes = {}
         w_scales = {}
         for g, t in [(0, 0), (0, 1), (1, 0), (1, 1), (0, 2), (1, 2), (0, 3), (1, 3)]:
@@ -121,11 +108,11 @@ def tile_picked_inorm_none_e_kernel(tc, xT, w1, w2_words, w2_scales, gamma, offs
             nc.vector.quantize_mx(
                 out=codes[:].bitcast(FP8X4),
                 scales=w_scales[g, t],
-                in_=w_grouped[g][:, t].rearrange("p m j -> p (m j)"),
+                in_=w_grouped[g, t // 2][:, t % 2].rearrange("p m j -> p (m j)"),
             )
             w_codes[g, t] = codes
 
-        pieces = {t: [(0, S)] if t in (1, 2) else [(0, S // 2), (S // 2, S)] for t in range(PACK)}
+        pieces = {t: [(0, S)] if t == 1 else [(0, S // 2), (S // 2, S)] for t in range(PACK)}
         banks = {(t, a): psum.tile([P, b - a], F32, name=f"h_{t}_{a}", tag=f"h_{t}_{a}") for t in range(PACK) for a, b in pieces[t]}
         for g, t in [(0, 0), (0, 1), (1, 0), (1, 1), (0, 2), (1, 2), (0, 3), (1, 3)]:
             for a, b in pieces[t]:
@@ -134,7 +121,7 @@ def tile_picked_inorm_none_e_kernel(tc, xT, w1, w2_words, w2_scales, gamma, offs
                     lhsT=w_codes[g, t][:].bitcast(FP8X4),
                     lhsT_scale=w_scales[g, t],
                     rhs=picked[g][:, a:b].bitcast(FP8X4),
-                    rhs_scale=picked_scales[4 * g : P, a:b],
+                    rhs_scale=picked_scales[g][:, a:b],
                     start=(g == 0),
                     stop=(g == PASSES - 1),
                 )
@@ -185,8 +172,10 @@ def tile_picked_inorm_none_e_kernel(tc, xT, w1, w2_words, w2_scales, gamma, offs
         inverse_root(0, 1)
         statistics(2, 0)
         aggregate(1)
-        scaled_mean(0, 1)
         copy_out(2, 0)
+        statistics(2, 1)
+        scaled_mean(0, 1)
+        copy_out(2, 1)
         statistics(3, 0)
         aggregate(2)
         inverse_root(1, 3)
@@ -207,7 +196,7 @@ def tile_picked_inorm_none_e_kernel(tc, xT, w1, w2_words, w2_scales, gamma, offs
         weave_z(False, 3, 0, 64)
         weave_z(True, 2)
         weave_z(True, 3, 64, P)
-        acc_tags = {1: ("h_0_0", "h_0_256"), 2: ("h_2_0", "h_3_0"), 3: ("spare_0", "spare_1")}
+        acc_tags = {1: ("h_0_0", "h_0_256"), 2: ("h_2_0", "h_3_0"), 3: ("h_2_256", "spare_1")}
         out_rows = out.rearrange("(b p) n -> p b n", p=P)
         for h in range(4):
             z_codes = keep.tile([P, P], U32, name=f"z_codes_{h}", align_bytes=64)

@@ -69,22 +69,31 @@ def tile_picked_inorm_none_e_kernel(tc, xT, w1, w2_words, w2_scales, gamma, offs
 
         picked = []
         picked_scales = []
-        x_on_vector = [[688,544],[208,224]]
+        x_on_vector = [[688,688],[256,368]]
         for g in range(PASSES):
-            grouped = keep.tile([P, S, PACK], BF16, name=f"x_grouped_{g}", align_bytes=64)
-            grouped_words = grouped[:].rearrange("p n j -> p (n j)").bitcast(U32).rearrange("p (n u) -> p n u", u=2)
+            found = [keep.tile([P, 2, S // 2], U32, name=f"x_found_{g}_{n}", align_bytes=64) for n in range(2)]
+            spans = [(0, S // 2), (S // 2, S)]
             for u in range(2):
                 cut = x_on_vector[g][u]
                 pairs = keep.tile([P, T], U32, name=f"x_pairs_{g}_{u}", align_bytes=64)
                 halves = pairs[:].bitcast(BF16).rearrange("p (n j) -> p n j", j=2)
                 weave(False, halves[:, cut:T, :], x_raw[g, u][:, :, cut:T])
                 weave(True, halves[:, 0:cut, :], x_raw[g, u][:, :, 0:cut])
-                nc.vector.tensor_copy(out=grouped_words[:, :, u], in_=pairs[:].indirect(offsets[:]))
+                for n, (a, b) in enumerate(spans):
+                    nc.vector.tensor_copy(out=found[n][:, u, :], in_=pairs[:].indirect(offsets[:, a // 16 : b // 16]))
             codes = keep.tile([P, S], U32, name=f"picked_{g}", align_bytes=64)
             scales = keep.tile([P, S], U8, name=f"picked_scales_{g}", align_bytes=64)
-            nc.vector.quantize_mx(out=codes[:].bitcast(FP8X4), scales=scales[:], in_=grouped[:].rearrange("p n j -> p (n j)"))
+            grouped = [keep.tile([P, S // 2, 2], I32, name=f"x_grouped_{g}_{n}", align_bytes=64) for n in range(2)]
+            for n in range(2):
+                weave(True, grouped[n][:], found[n][:].bitcast(I32))
+            for n in range(2):
+                nc.vector.quantize_mx(out=codes[:, n * S // 2 : (n + 1) * S // 2].bitcast(FP8X4), scales=scales[:, n * S // 2 : (n + 1) * S // 2], in_=grouped[n][:].rearrange("p n u -> p (n u)").bitcast(BF16))
             picked.append(codes)
             picked_scales.append(scales)
+
+        warm_bank = psum.tile([P, S], F32, name="warm_bank", tag="spare_1")
+        for n in range(1):
+            nc.tensor.matmul_mx(out=warm_bank[:], lhsT=picked[1][:, 0:P].bitcast(FP8X4), lhsT_scale=picked_scales[1][:, 0:P], rhs=picked[0][:].bitcast(FP8X4), rhs_scale=picked_scales[0][:], start=True, stop=True)
 
         w_grouped = {}
         for g in range(PASSES):
@@ -92,38 +101,33 @@ def tile_picked_inorm_none_e_kernel(tc, xT, w1, w2_words, w2_scales, gamma, offs
                 w_grouped[g, u] = keep.tile([P, 2, P, PACK], BF16, name=f"w_grouped_{g}_{u}", align_bytes=64)
                 dst = w_grouped[g, u][:].rearrange("p t m j -> p m j t")
                 src = w_raw[g][:].rearrange("p j (m t) -> p m j t", t=PACK)[:, :, :, 2 * u : 2 * u + 2]
-                cut = [[128,128],[60,88]][g][u]
+                cut = [[128,128],[56,64]][g][u]
                 cast(False, dst[:, 0:cut], src[:, 0:cut])
                 if cut < P:
                     cast(True, dst[:, cut:P], src[:, cut:P])
         w_codes = {}
         w_scales = {}
-        for g, t in [(0, 0), (0, 1), (1, 0), (1, 1), (0, 2), (1, 2), (0, 3), (1, 3)]:
-            codes = keep.tile([P, P], U32, name=f"w_codes_{g}_{t}", align_bytes=64)
-            if g == 0 and t >= 2:
-                w_scales[g, t] = plane[4:P, :]
-            else:
-                plane = keep.tile([P, P], U8, name=f"w_scales_{g}_{t}", align_bytes=64)
-                w_scales[g, t] = plane[:]
-            nc.vector.quantize_mx(
-                out=codes[:].bitcast(FP8X4),
-                scales=w_scales[g, t],
-                in_=w_grouped[g, t // 2][:, t % 2].rearrange("p m j -> p (m j)"),
-            )
-            w_codes[g, t] = codes
+        for g in range(PASSES):
+            for u in range(2):
+                codes = keep.tile([P, 2 * P], U32, name=f"w_codes_{g}_{u}", align_bytes=64)
+                plane = keep.tile([P, 2 * P], U8, name=f"w_scales_{g}_{u}", align_bytes=64)
+                nc.vector.quantize_mx(out=codes[:].bitcast(FP8X4), scales=plane[:], in_=w_grouped[g, u][:].rearrange("p t m j -> p (t m j)"))
+                for t in range(2):
+                    w_codes[g, 2 * u + t] = codes[:, t * P : (t + 1) * P]
+                    w_scales[g, 2 * u + t] = plane[:, t * P : (t + 1) * P]
 
         pieces = {t: [(0, S)] if t == 1 else [(0, S // 2), (S // 2, S)] for t in range(PACK)}
         banks = {(t, a): psum.tile([P, b - a], F32, name=f"h_{t}_{a}", tag=f"h_{t}_{a}") for t in range(PACK) for a, b in pieces[t]}
-        for g, t in [(0, 0), (0, 1), (1, 0), (1, 1), (0, 2), (1, 2), (0, 3), (1, 3)]:
+        for g, t in [(0, 0), (0, 1), (1, 0), (1, 1), (1, 2), (0, 2), (1, 3), (0, 3)]:
             for a, b in pieces[t]:
                 nc.tensor.matmul_mx(
                     out=banks[t, a][:],
-                    lhsT=w_codes[g, t][:].bitcast(FP8X4),
+                    lhsT=w_codes[g, t].bitcast(FP8X4),
                     lhsT_scale=w_scales[g, t],
                     rhs=picked[g][:, a:b].bitcast(FP8X4),
                     rhs_scale=picked_scales[g][:, a:b],
-                    start=(g == 0),
-                    stop=(g == PASSES - 1),
+                    start=(g == t // 2),
+                    stop=(g != t // 2),
                 )
 
         z_planes = keep.tile([P, PACK, S], BF16, name="z_planes", align_bytes=64)

@@ -52,14 +52,14 @@ def tile_picked_inorm_none_e_kernel(tc, xT, w1, w2_words, w2_scales, gamma, offs
         for g in range(PASSES):
             rows = xT[g * K_PASS : (g + 1) * K_PASS, :].rearrange("(p j) n -> p j n", j=PACK)
             for u in range(2):
-                x_raw[g, u] = keep.tile([P, 2, T], F32, name=f"x_raw_{g}_{u}")
+                x_raw[g, u] = keep.tile([P, 2, T], F32, name=f"x_raw_{g}_{u}", tag=f"x_raw_{g}_{u}", align_bytes=64)
                 nc.sync.dma_start(out=x_raw[g, u][:], in_=rows[:, 2 * u : 2 * u + 2, :])
                 if (g, u) == (0, 0):
                     nc.sync.dma_start(offsets[:], offs)
 
         w_raw = []
         for g in range(PASSES):
-            raw = keep.tile([P, PACK, H], F32, name=f"w_raw_{g}")
+            raw = keep.tile([P, PACK, H], F32, name=f"w_raw_{g}", tag=f"w_raw_{g}", align_bytes=64)
             nc.sync.dma_start(out=raw[:], in_=w1[g * K_PASS : (g + 1) * K_PASS, :].rearrange("(p j) n -> p j n", j=PACK))
             w_raw.append(raw)
         nc.sync.dma_start(out=gam[:], in_=gamma.rearrange("(p t) o -> p (t o)", t=PACK))
@@ -67,31 +67,47 @@ def tile_picked_inorm_none_e_kernel(tc, xT, w1, w2_words, w2_scales, gamma, offs
         for q in range(4):
             nc.sync.dma_start(out=w2_plane[32 * q : 32 * q + 4, :].bitcast(I32), in_=w2_scales[0, 4 * q : 4 * q + 4, :].bitcast(I32))
 
-        picked = []
-        picked_scales = []
-        x_on_vector = [[688,688],[256,368]]
-        for g in range(PASSES):
-            found = [keep.tile([P, 2, S // 2], U32, name=f"x_found_{g}_{n}", align_bytes=64) for n in range(2)]
-            spans = [(0, S // 2), (S // 2, S)]
-            for u in range(2):
-                cut = x_on_vector[g][u]
-                pairs = keep.tile([P, T], U32, name=f"x_pairs_{g}_{u}", align_bytes=64)
-                halves = pairs[:].bitcast(BF16).rearrange("p (n j) -> p n j", j=2)
-                weave(False, halves[:, cut:T, :], x_raw[g, u][:, :, cut:T])
-                weave(True, halves[:, 0:cut, :], x_raw[g, u][:, :, 0:cut])
-                for n, (a, b) in enumerate(spans):
-                    nc.vector.tensor_copy(out=found[n][:, u, :], in_=pairs[:].indirect(offsets[:, a // 16 : b // 16]))
-            codes = keep.tile([P, S], U32, name=f"picked_{g}", align_bytes=64)
-            scales = keep.tile([P, S], U8, name=f"picked_scales_{g}", align_bytes=64)
-            grouped = [keep.tile([P, S // 2, 2], I32, name=f"x_grouped_{g}_{n}", align_bytes=64) for n in range(2)]
-            for n in range(2):
-                weave(True, grouped[n][:], found[n][:].bitcast(I32))
-            for n in range(2):
-                nc.vector.quantize_mx(out=codes[:, n * S // 2 : (n + 1) * S // 2].bitcast(FP8X4), scales=scales[:, n * S // 2 : (n + 1) * S // 2], in_=grouped[n][:].rearrange("p n u -> p (n u)").bitcast(BF16))
-            picked.append(codes)
-            picked_scales.append(scales)
+        x_on_vector = [[688,688],[656,480]]
+        found = [keep.tile([P, 2, S], U32, name=f"x_found_{g}", align_bytes=64) for g in range(PASSES)]
+        grouped = {}
+        picked = {}
+        picked_scales = {}
 
-        warm_bank = psum.tile([P, S], F32, name="warm_bank", tag="spare_1")
+        def look_up(g, u):
+            cut = x_on_vector[g][u]
+            pairs = keep.tile([P, T], U32, name=f"x_pairs_{g}_{u}", align_bytes=64)
+            halves = pairs[:].bitcast(BF16).rearrange("p (n j) -> p n j", j=2)
+            weave(False, halves[:, cut:T, :], x_raw[g, u][:, :, cut:T])
+            weave(True, halves[:, 0:cut, :], x_raw[g, u][:, :, 0:cut])
+            for a, b in [(0, S // 2), (S // 2, S)] if (g, u) == (1, 1) else [(0, S)]:
+                nc.vector.tensor_copy(out=found[g][:, u, a:b], in_=pairs[:].indirect(offsets[:, a // 16 : b // 16]))
+
+        def join(g):
+            both = keep.tile([P, 2, S // 2, 2], U32, name=f"x_grouped_{g}", tag="x_raw_1_0" if g == 0 else "x_grouped_1", align_bytes=64)
+            grouped[g] = [both[:, n] for n in range(2)]
+            for n in range(2):
+                if g == 0:
+                    nc.scalar.copy(out=grouped[g][n].rearrange("p (c i) t -> p c t i", i=4), in_=found[g][:, :, n * S // 2 : (n + 1) * S // 2].rearrange("p t (c i) -> p c t i", i=4))
+                else:
+                    weave(True, grouped[g][n].bitcast(I32), found[g][:, :, n * S // 2 : (n + 1) * S // 2].bitcast(I32))
+
+        def quantise_points(g):
+            picked[g] = keep.tile([P, S], U32, name=f"picked_{g}", align_bytes=64)
+            picked_scales[g] = keep.tile([P, S], U8, name=f"picked_scales_{g}", align_bytes=64)
+            for n in range(2):
+                cols = slice(n * S // 2, (n + 1) * S // 2)
+                nc.vector.quantize_mx(out=picked[g][:, cols].bitcast(FP8X4), scales=picked_scales[g][:, cols], in_=grouped[g][n].rearrange("p n u -> p (n u)").bitcast(BF16))
+
+        look_up(0, 0)
+        look_up(0, 1)
+        look_up(1, 0)
+        join(0)
+        quantise_points(0)
+        look_up(1, 1)
+        join(1)
+        quantise_points(1)
+
+        warm_bank = psum.tile([P, S], F32, name="warm_bank", tag="h_3_256")
         for n in range(1):
             nc.tensor.matmul_mx(out=warm_bank[:], lhsT=picked[1][:, 0:P].bitcast(FP8X4), lhsT_scale=picked_scales[1][:, 0:P], rhs=picked[0][:].bitcast(FP8X4), rhs_scale=picked_scales[0][:], start=True, stop=True)
 
@@ -101,33 +117,37 @@ def tile_picked_inorm_none_e_kernel(tc, xT, w1, w2_words, w2_scales, gamma, offs
                 w_grouped[g, u] = keep.tile([P, 2, P, PACK], BF16, name=f"w_grouped_{g}_{u}", align_bytes=64)
                 dst = w_grouped[g, u][:].rearrange("p t m j -> p m j t")
                 src = w_raw[g][:].rearrange("p j (m t) -> p m j t", t=PACK)[:, :, :, 2 * u : 2 * u + 2]
-                cut = [[128,128],[56,64]][g][u]
+                cut = [[128,128],[48,48]][g][u]
                 cast(False, dst[:, 0:cut], src[:, 0:cut])
                 if cut < P:
                     cast(True, dst[:, cut:P], src[:, cut:P])
         w_codes = {}
         w_scales = {}
-        for g in range(PASSES):
-            for u in range(2):
-                codes = keep.tile([P, 2 * P], U32, name=f"w_codes_{g}_{u}", align_bytes=64)
+        for g, u in [(0, 0), (1, 0), (1, 1), (0, 1)]:
+            if True:
+                codes = keep.tile([P, 2 * P], U32, name=f"w_codes_{g}_{u}", tag="w_raw_1" if (g, u) == (0, 1) else f"w_codes_{g}_{u}", align_bytes=64)
                 plane = keep.tile([P, 2 * P], U8, name=f"w_scales_{g}_{u}", align_bytes=64)
-                nc.vector.quantize_mx(out=codes[:].bitcast(FP8X4), scales=plane[:], in_=w_grouped[g, u][:].rearrange("p t m j -> p (t m j)"))
+                for t0, t1 in [(0, 1), (1, 2)] if (g, u) == (1, 0) else [(0, 2)]:
+                    nc.vector.quantize_mx(out=codes[:, t0 * P : t1 * P].bitcast(FP8X4), scales=plane[:, t0 * P : t1 * P], in_=w_grouped[g, u][:, t0:t1].rearrange("p t m j -> p (t m j)"))
                 for t in range(2):
                     w_codes[g, 2 * u + t] = codes[:, t * P : (t + 1) * P]
                     w_scales[g, 2 * u + t] = plane[:, t * P : (t + 1) * P]
 
-        pieces = {t: [(0, S)] if t == 1 else [(0, S // 2), (S // 2, S)] for t in range(PACK)}
+        pieces = {t: [(0, S // 2), (S // 2, S)] for t in range(PACK)}
         banks = {(t, a): psum.tile([P, b - a], F32, name=f"h_{t}_{a}", tag=f"h_{t}_{a}") for t in range(PACK) for a, b in pieces[t]}
-        for g, t in [(0, 0), (0, 1), (1, 0), (1, 1), (1, 2), (0, 2), (1, 3), (0, 3)]:
-            for a, b in pieces[t]:
+        early = [(t, a, b) for t in range(PACK) for a, b in pieces[t]][:3]
+        late = [(t, a, b) for t in range(PACK) for a, b in pieces[t]][3:]
+        passes = [(0, x, True) for x in early] + [(1, x, False) for x in early] + [(g, x, g == 1) for x in late for g in (1, 0)]
+        for g, (t, a, b), first in passes:
+            if True:
                 nc.tensor.matmul_mx(
                     out=banks[t, a][:],
                     lhsT=w_codes[g, t].bitcast(FP8X4),
                     lhsT_scale=w_scales[g, t],
                     rhs=picked[g][:, a:b].bitcast(FP8X4),
                     rhs_scale=picked_scales[g][:, a:b],
-                    start=(g == t // 2),
-                    stop=(g != t // 2),
+                    start=first,
+                    stop=not first,
                 )
 
         z_planes = keep.tile([P, PACK, S], BF16, name="z_planes", align_bytes=64)
@@ -138,13 +158,19 @@ def tile_picked_inorm_none_e_kernel(tc, xT, w1, w2_words, w2_scales, gamma, offs
         h_copy = [keep.tile([P, S], F32, name=f"h_copy_{t}") for t in range(PACK)]
         z_grouped = [keep.tile([P, P, PACK], BF16, name=f"z_grouped_{h}", align_bytes=64) for h in range(4)]
 
+        minus_gam = keep.tile([P, 1], F32, name="minus_gam")
+        nc.vector.tensor_scalar(out=minus_gam[:], in0=gam[:, 3:4], scalar1=-1.0, scalar2=0.0, op0=ALU.mult, op1=ALU.add)
+
         def statistics(t, n):
             a, b = pieces[t][n]
             nc.vector.bn_stats(out=stats[t][:, 6 * n : 6 * n + 6], in_=banks[t, a][:])
 
         def copy_out(t, n):
             a, b = pieces[t][n]
-            nc.scalar.activation(out=h_copy[t][:, a:b], in_=banks[t, a][:], func=ACT.Copy, scale=gam[:, t : t + 1])
+            if (t, n) == (3, 1):
+                nc.scalar.activation(out=h_copy[t][:, a:b], in_=banks[t, a][:], func=ACT.Identity, scale=-1.0, bias=moments[:, t, 0:1])
+            else:
+                nc.scalar.activation(out=h_copy[t][:, a:b], in_=banks[t, a][:], func=ACT.Copy, scale=gam[:, t : t + 1])
 
         def aggregate(t):
             nc.vector.bn_aggr(out=moments[:, t, :], in_=stats[t][:])
@@ -153,9 +179,12 @@ def tile_picked_inorm_none_e_kernel(tc, xT, w1, w2_words, w2_scales, gamma, offs
             nc.scalar.activation(out=rstd[:, t0:t1], in_=moments[:, t0:t1, 1], func=ACT.Abs_reciprocal_sqrt, bias=EPS)
 
         def scaled_mean(t0, t1):
-            nc.vector.tensor_tensor(out=shift[:, t0:t1], in0=moments[:, t0:t1, 0], in1=gam[:, t0:t1], op=ALU.mult)
+            nc.scalar.activation(out=shift[:, t0:t1], in_=moments[:, t0:t1, 0], func=ACT.Copy, scale=gam[:, t0:t1])
 
         def normalise(t, a, b):
+            if (t, a) == (3, S // 2):
+                nc.vector.tensor_scalar(out=z_planes[:, t, a:b], in0=h_copy[t][:, a:b], scalar1=rstd[:, t : t + 1], scalar2=minus_gam[:, 0:1], op0=ALU.mult, op1=ALU.mult)
+                return
             nc.vector.tensor_scalar(out=z_planes[:, t, a:b], in0=h_copy[t][:, a:b], scalar1=shift[:, t : t + 1], scalar2=rstd[:, t : t + 1], op0=ALU.subtract, op1=ALU.mult)
 
         def weave_z(on_vector, h, a=0, b=P):
@@ -166,32 +195,36 @@ def tile_picked_inorm_none_e_kernel(tc, xT, w1, w2_words, w2_scales, gamma, offs
             else:
                 nc.scalar.copy(out=dst, in_=src)
 
-        statistics(0, 0)
-        copy_out(0, 0)
-        statistics(0, 1)
         copy_out(0, 1)
+        statistics(0, 0)
+        copy_out(1, 1)
         statistics(1, 0)
-        aggregate(0)
+        statistics(0, 1)
+        copy_out(0, 0)
         copy_out(1, 0)
+        statistics(1, 1)
+        aggregate(0)
         inverse_root(0, 1)
+        scaled_mean(0, 1)
         statistics(2, 0)
         aggregate(1)
         copy_out(2, 0)
+        inverse_root(1, 2)
+        scaled_mean(1, 2)
         statistics(2, 1)
-        scaled_mean(0, 1)
         copy_out(2, 1)
         statistics(3, 0)
         aggregate(2)
-        inverse_root(1, 3)
+        inverse_root(2, 3)
+        scaled_mean(2, 3)
         copy_out(3, 0)
         statistics(3, 1)
-        scaled_mean(1, 3)
         normalise(0, 0, S)
         aggregate(3)
         inverse_root(3, 4)
+        scaled_mean(3, 4)
         copy_out(3, 1)
         normalise(1, 0, S)
-        scaled_mean(3, 4)
         normalise(2, 0, S)
         normalise(3, 0, 256)
         weave_z(False, 1)
@@ -200,7 +233,7 @@ def tile_picked_inorm_none_e_kernel(tc, xT, w1, w2_words, w2_scales, gamma, offs
         weave_z(False, 3, 0, 64)
         weave_z(True, 2)
         weave_z(True, 3, 64, P)
-        acc_tags = {1: ("h_0_0", "h_0_256"), 2: ("h_2_0", "h_3_0"), 3: ("h_2_256", "spare_1")}
+        acc_tags = {1: ("h_0_0", "h_0_256"), 2: ("h_2_0", "h_3_0"), 3: ("h_2_256", "h_1_256")}
         out_rows = out.rearrange("(b p) n -> p b n", p=P)
         for h in range(4):
             z_codes = keep.tile([P, P], U32, name=f"z_codes_{h}", align_bytes=64)

@@ -19,245 +19,257 @@ P = 128
 PACK = 4
 K_PASS = P * PACK
 PASSES = K // K_PASS
+HALF = S // 2
+QUARTER = S // 4
+LAST = PACK - 1
 EPS = 1e-5
+ALIGN = 64
+
+X_ON_VECTOR = ((688, 688), (656, 480))
+W_ON_SCALAR = ((P, P), (64, 48))
 
 
 def tile_picked_inorm_none_e_kernel(tc, xT, w1, w2_words, w2_scales, gamma, offs, out):
     nc = tc.nc
 
-    def cast(on_vector, dst, src):
+    def copy_floats(on_vector, dst, src):
         if on_vector:
             nc.vector.tensor_copy(out=dst, in_=src)
         else:
             nc.scalar.activation(out=dst, in_=src, func=ACT.Copy)
 
-    def weave(on_vector, dst, src):
-        cast(on_vector, dst.rearrange("p (c i) t -> p c t i", i=4), src.rearrange("p t (c i) -> p c t i", i=4))
+    def copy_bits(on_vector, dst, src):
+        if on_vector:
+            nc.vector.tensor_copy(out=dst, in_=src)
+        else:
+            nc.scalar.copy(out=dst, in_=src)
+
+    def interleave(copy, on_vector, dst, src):
+        copy(on_vector, dst.rearrange("p (c i) r -> p c r i", i=4), src.rearrange("p r (c i) -> p c r i", i=4))
 
     with ExitStack() as ctx:
         keep = ctx.enter_context(tc.tile_pool(name="keep", bufs=1))
         psum = ctx.enter_context(tc.psum_pool(name="psum", bufs=1))
 
         offsets = keep.tile([P, S // 16], U16, name="offsets")
-        w2_codes = keep.tile([P, N], U32, name="w2_codes", align_bytes=64)
-        w2_plane = keep.tile([P, N], U8, name="w2_plane", align_bytes=64)
+        w2_codes = keep.tile([P, N], U32, name="w2_codes", align_bytes=ALIGN)
+        w2_plane = keep.tile([P, N], U8, name="w2_plane", align_bytes=ALIGN)
         gam = keep.tile([P, PACK], F32, name="gam")
-        warm = keep.tile([P, 2], F32, name="warm")
+        preload = keep.tile([P, 2], F32, name="preload")
 
         nc.vector.memset(w2_plane[:].bitcast(U32), 0)
-        nc.vector.memset(warm[:, 0:1], 1.0)
-        nc.scalar.activation(out=warm[:, 1:2], in_=warm[:, 0:1], func=ACT.Abs_reciprocal_sqrt)
+        nc.vector.memset(preload[:, 0:1], 1.0)
+        nc.scalar.activation(out=preload[:, 1:2], in_=preload[:, 0:1], func=ACT.Abs_reciprocal_sqrt)
 
         x_raw = {}
         for g in range(PASSES):
             rows = xT[g * K_PASS : (g + 1) * K_PASS, :].rearrange("(p j) n -> p j n", j=PACK)
             for u in range(2):
-                x_raw[g, u] = keep.tile([P, 2, T], F32, name=f"x_raw_{g}_{u}", tag=f"x_raw_{g}_{u}", align_bytes=64)
+                x_raw[g, u] = keep.tile([P, 2, T], F32, name=f"x_raw_{g}_{u}", align_bytes=ALIGN)
                 nc.sync.dma_start(out=x_raw[g, u][:], in_=rows[:, 2 * u : 2 * u + 2, :])
                 if (g, u) == (0, 0):
                     nc.sync.dma_start(offsets[:], offs)
-
-        w_raw = []
+        w_raw = {}
         for g in range(PASSES):
-            raw = keep.tile([P, PACK, H], F32, name=f"w_raw_{g}", tag=f"w_raw_{g}", align_bytes=64)
-            nc.sync.dma_start(out=raw[:], in_=w1[g * K_PASS : (g + 1) * K_PASS, :].rearrange("(p j) n -> p j n", j=PACK))
-            w_raw.append(raw)
+            w_raw[g] = keep.tile([P, PACK, H], F32, name=f"w_raw_{g}", align_bytes=ALIGN)
+            nc.sync.dma_start(out=w_raw[g][:], in_=w1[g * K_PASS : (g + 1) * K_PASS, :].rearrange("(p j) n -> p j n", j=PACK))
         nc.sync.dma_start(out=gam[:], in_=gamma.rearrange("(p t) o -> p (t o)", t=PACK))
-        nc.sync.dma_start(out=w2_codes[:].bitcast(I32), in_=w2_words[0].rearrange("p n t -> p (n t)").bitcast(I32))
+        nc.sync.dma_start(out=w2_codes[:].bitcast(I32), in_=w2_words[0].rearrange("p n j -> p (n j)").bitcast(I32))
         for q in range(4):
             nc.sync.dma_start(out=w2_plane[32 * q : 32 * q + 4, :].bitcast(I32), in_=w2_scales[0, 4 * q : 4 * q + 4, :].bitcast(I32))
 
-        x_on_vector = [[688,688],[656,480]]
-        found = [keep.tile([P, 2, S], U32, name=f"x_found_{g}", align_bytes=64) for g in range(PASSES)]
-        grouped = {}
-        picked = {}
-        picked_scales = {}
+        found = [keep.tile([P, 2, S], U32, name=f"x_found_{g}", align_bytes=ALIGN) for g in range(PASSES)]
+        joined = {}
+        x_codes = {}
+        x_scales = {}
 
-        def look_up(g, u):
-            cut = x_on_vector[g][u]
-            pairs = keep.tile([P, T], U32, name=f"x_pairs_{g}_{u}", align_bytes=64)
-            halves = pairs[:].bitcast(BF16).rearrange("p (n j) -> p n j", j=2)
-            weave(False, halves[:, cut:T, :], x_raw[g, u][:, :, cut:T])
-            weave(True, halves[:, 0:cut, :], x_raw[g, u][:, :, 0:cut])
-            for a, b in [(0, S // 2), (S // 2, S)] if (g, u) == (1, 1) else [(0, S)]:
+        def look_up(g, u, spans):
+            cut = X_ON_VECTOR[g][u]
+            pairs = keep.tile([P, T], U32, name=f"x_pairs_{g}_{u}", align_bytes=ALIGN)
+            values = pairs[:].bitcast(BF16).rearrange("p (n j) -> p n j", j=2)
+            interleave(copy_floats, False, values[:, cut:T, :], x_raw[g, u][:, :, cut:T])
+            interleave(copy_floats, True, values[:, 0:cut, :], x_raw[g, u][:, :, 0:cut])
+            for a, b in spans:
                 nc.vector.tensor_copy(out=found[g][:, u, a:b], in_=pairs[:].indirect(offsets[:, a // 16 : b // 16]))
 
-        def join(g):
-            both = keep.tile([P, 2, S // 2, 2], U32, name=f"x_grouped_{g}", tag="x_raw_1_0" if g == 0 else "x_grouped_1", align_bytes=64)
-            grouped[g] = [both[:, n] for n in range(2)]
+        def join(g, on_vector, tag):
+            joined[g] = keep.tile([P, 2, HALF, 2], U32, name=f"x_joined_{g}", tag=tag, align_bytes=ALIGN)
+            view = I32 if on_vector else U32
             for n in range(2):
-                if g == 0:
-                    nc.scalar.copy(out=grouped[g][n].rearrange("p (c i) t -> p c t i", i=4), in_=found[g][:, :, n * S // 2 : (n + 1) * S // 2].rearrange("p t (c i) -> p c t i", i=4))
-                else:
-                    weave(True, grouped[g][n].bitcast(I32), found[g][:, :, n * S // 2 : (n + 1) * S // 2].bitcast(I32))
+                interleave(copy_bits, on_vector, joined[g][:, n].bitcast(view), found[g][:, :, n * HALF : (n + 1) * HALF].bitcast(view))
 
-        def quantise_points(g):
-            picked[g] = keep.tile([P, S], U32, name=f"picked_{g}", align_bytes=64)
-            picked_scales[g] = keep.tile([P, S], U8, name=f"picked_scales_{g}", align_bytes=64)
-            for n in range(2):
-                cols = slice(n * S // 2, (n + 1) * S // 2)
-                nc.vector.quantize_mx(out=picked[g][:, cols].bitcast(FP8X4), scales=picked_scales[g][:, cols], in_=grouped[g][n].rearrange("p n u -> p (n u)").bitcast(BF16))
+        def quantise_points(g, n, tag):
+            x_codes[g, n] = keep.tile([P, HALF], U32, name=f"x_codes_{g}_{n}", tag=tag, align_bytes=ALIGN)
+            x_scales[g, n] = keep.tile([P, HALF], U8, name=f"x_scales_{g}_{n}", align_bytes=ALIGN)
+            nc.vector.quantize_mx(
+                out=x_codes[g, n][:].bitcast(FP8X4),
+                scales=x_scales[g, n][:],
+                in_=joined[g][:, n].rearrange("p n u -> p (n u)").bitcast(BF16),
+            )
 
-        look_up(0, 0)
-        look_up(0, 1)
-        look_up(1, 0)
-        join(0)
-        quantise_points(0)
-        look_up(1, 1)
-        join(1)
-        quantise_points(1)
-
-        warm_bank = psum.tile([P, S], F32, name="warm_bank", tag="h_3_256")
-        for n in range(1):
-            nc.tensor.matmul_mx(out=warm_bank[:], lhsT=picked[1][:, 0:P].bitcast(FP8X4), lhsT_scale=picked_scales[1][:, 0:P], rhs=picked[0][:].bitcast(FP8X4), rhs_scale=picked_scales[0][:], start=True, stop=True)
-
-        w_grouped = {}
-        for g in range(PASSES):
-            for u in range(2):
-                w_grouped[g, u] = keep.tile([P, 2, P, PACK], BF16, name=f"w_grouped_{g}_{u}", align_bytes=64)
-                dst = w_grouped[g, u][:].rearrange("p t m j -> p m j t")
-                src = w_raw[g][:].rearrange("p j (m t) -> p m j t", t=PACK)[:, :, :, 2 * u : 2 * u + 2]
-                cut = [[128,128],[48,48]][g][u]
-                cast(False, dst[:, 0:cut], src[:, 0:cut])
-                if cut < P:
-                    cast(True, dst[:, cut:P], src[:, cut:P])
+        dealt = {}
         w_codes = {}
         w_scales = {}
-        for g, u in [(0, 0), (1, 0), (1, 1), (0, 1)]:
-            if True:
-                codes = keep.tile([P, 2 * P], U32, name=f"w_codes_{g}_{u}", tag="w_raw_1" if (g, u) == (0, 1) else f"w_codes_{g}_{u}", align_bytes=64)
-                plane = keep.tile([P, 2 * P], U8, name=f"w_scales_{g}_{u}", align_bytes=64)
-                for t0, t1 in [(0, 1), (1, 2)] if (g, u) == (1, 0) else [(0, 2)]:
-                    nc.vector.quantize_mx(out=codes[:, t0 * P : t1 * P].bitcast(FP8X4), scales=plane[:, t0 * P : t1 * P], in_=w_grouped[g, u][:, t0:t1].rearrange("p t m j -> p (t m j)"))
-                for t in range(2):
-                    w_codes[g, 2 * u + t] = codes[:, t * P : (t + 1) * P]
-                    w_scales[g, 2 * u + t] = plane[:, t * P : (t + 1) * P]
 
-        pieces = {t: [(0, S // 2), (S // 2, S)] for t in range(PACK)}
-        banks = {(t, a): psum.tile([P, b - a], F32, name=f"h_{t}_{a}", tag=f"h_{t}_{a}") for t in range(PACK) for a, b in pieces[t]}
-        early = [(t, a, b) for t in range(PACK) for a, b in pieces[t]][:3]
-        late = [(t, a, b) for t in range(PACK) for a, b in pieces[t]][3:]
-        passes = [(0, x, True) for x in early] + [(1, x, False) for x in early] + [(g, x, g == 1) for x in late for g in (1, 0)]
-        for g, (t, a, b), first in passes:
-            if True:
-                nc.tensor.matmul_mx(
-                    out=banks[t, a][:],
-                    lhsT=w_codes[g, t].bitcast(FP8X4),
-                    lhsT_scale=w_scales[g, t],
-                    rhs=picked[g][:, a:b].bitcast(FP8X4),
-                    rhs_scale=picked_scales[g][:, a:b],
-                    start=first,
-                    stop=not first,
+        def deal_weights(g, u):
+            cut = W_ON_SCALAR[g][u]
+            dealt[g, u] = keep.tile([P, 2, P, PACK], BF16, name=f"w_dealt_{g}_{u}", align_bytes=ALIGN)
+            dst = dealt[g, u][:].rearrange("p s m j -> p m j s")
+            src = w_raw[g][:].rearrange("p j (m t) -> p m j t", t=PACK)[:, :, :, 2 * u : 2 * u + 2]
+            copy_floats(False, dst[:, 0:cut], src[:, 0:cut])
+            if cut < P:
+                copy_floats(True, dst[:, cut:P], src[:, cut:P])
+
+        def quantise_weights(g, u, spans, tag):
+            codes = keep.tile([P, 2 * P], U32, name=f"w_codes_{g}_{u}", tag=tag, align_bytes=ALIGN)
+            plane = keep.tile([P, 2 * P], U8, name=f"w_scales_{g}_{u}", align_bytes=ALIGN)
+            for s0, s1 in spans:
+                nc.vector.quantize_mx(
+                    out=codes[:, s0 * P : s1 * P].bitcast(FP8X4),
+                    scales=plane[:, s0 * P : s1 * P],
+                    in_=dealt[g, u][:, s0:s1].rearrange("p s m j -> p (s m j)"),
                 )
+            for s in range(2):
+                w_codes[g, 2 * u + s] = codes[:, s * P : (s + 1) * P]
+                w_scales[g, 2 * u + s] = plane[:, s * P : (s + 1) * P]
 
-        z_planes = keep.tile([P, PACK, S], BF16, name="z_planes", align_bytes=64)
-        stats = [keep.tile([P, 6 * len(pieces[t])], F32, name=f"stats_{t}") for t in range(PACK)]
+        whole_list = [(0, S)]
+        look_up(0, 0, whole_list)
+        look_up(0, 1, whole_list)
+        look_up(1, 0, whole_list)
+        join(0, False, "x_raw_1_0")
+        quantise_points(0, 0, "x_codes_0_0")
+        quantise_points(0, 1, "x_codes_0_1")
+        look_up(1, 1, [(0, HALF), (HALF, S)])
+        join(1, True, "x_joined_1")
+        quantise_points(1, 0, "x_codes_1_0")
+        for g in range(PASSES):
+            for u in range(2):
+                deal_weights(g, u)
+        both_tiles = [(0, 2)]
+        quantise_weights(0, 0, both_tiles, "w_codes_0_0")
+        quantise_points(1, 1, "w_dealt_0_0")
+        quantise_weights(1, 0, [(0, 1), (1, 2)], "w_codes_1_0")
+        quantise_weights(1, 1, both_tiles, "w_codes_1_1")
+        quantise_weights(0, 1, both_tiles, "w_raw_1")
+
+        banks = {(t, n): psum.tile([P, HALF], F32, name=f"h_{t}_{n}") for t in range(PACK) for n in range(2)}
+
+        def first_product(g, t, n, opens):
+            nc.tensor.matmul_mx(
+                out=banks[t, n][:],
+                lhsT=w_codes[g, t].bitcast(FP8X4),
+                lhsT_scale=w_scales[g, t],
+                rhs=x_codes[g, n][:].bitcast(FP8X4),
+                rhs_scale=x_scales[g, n][:],
+                start=opens,
+                stop=not opens,
+            )
+
+        for g in range(PASSES):
+            for t in (0, 1):
+                for n in range(2):
+                    first_product(g, t, n, g == 0)
+        for t in (2, 3):
+            for n in range(2):
+                for g in (1, 0):
+                    first_product(g, t, n, g == 1)
+
+        stats = [keep.tile([P, 2, 6], F32, name=f"stats_{t}") for t in range(PACK)]
         moments = keep.tile([P, PACK, 2], F32, name="moments")
         rstd = keep.tile([P, PACK], F32, name="rstd")
         shift = keep.tile([P, PACK], F32, name="shift")
-        h_copy = [keep.tile([P, S], F32, name=f"h_copy_{t}") for t in range(PACK)]
-        z_grouped = [keep.tile([P, P, PACK], BF16, name=f"z_grouped_{h}", align_bytes=64) for h in range(4)]
-
         minus_gam = keep.tile([P, 1], F32, name="minus_gam")
-        nc.vector.tensor_scalar(out=minus_gam[:], in0=gam[:, 3:4], scalar1=-1.0, scalar2=0.0, op0=ALU.mult, op1=ALU.add)
+        h_copy = [keep.tile([P, S], F32, name=f"h_copy_{t}") for t in range(PACK)]
+        z_planes = keep.tile([P, PACK, S], BF16, name="z_planes", align_bytes=ALIGN)
+        z_joined = [keep.tile([P, QUARTER, PACK], BF16, name=f"z_joined_{c}", align_bytes=ALIGN) for c in range(4)]
 
         def statistics(t, n):
-            a, b = pieces[t][n]
-            nc.vector.bn_stats(out=stats[t][:, 6 * n : 6 * n + 6], in_=banks[t, a][:])
+            nc.vector.bn_stats(out=stats[t][:, n, :], in_=banks[t, n][:])
 
         def copy_out(t, n):
-            a, b = pieces[t][n]
-            if (t, n) == (3, 1):
-                nc.scalar.activation(out=h_copy[t][:, a:b], in_=banks[t, a][:], func=ACT.Identity, scale=-1.0, bias=moments[:, t, 0:1])
-            else:
-                nc.scalar.activation(out=h_copy[t][:, a:b], in_=banks[t, a][:], func=ACT.Copy, scale=gam[:, t : t + 1])
+            nc.scalar.activation(out=h_copy[t][:, n * HALF : (n + 1) * HALF], in_=banks[t, n][:], func=ACT.Copy, scale=gam[:, t : t + 1])
 
-        def aggregate(t):
-            nc.vector.bn_aggr(out=moments[:, t, :], in_=stats[t][:])
-
-        def inverse_root(t0, t1):
-            nc.scalar.activation(out=rstd[:, t0:t1], in_=moments[:, t0:t1, 1], func=ACT.Abs_reciprocal_sqrt, bias=EPS)
-
-        def scaled_mean(t0, t1):
-            nc.scalar.activation(out=shift[:, t0:t1], in_=moments[:, t0:t1, 0], func=ACT.Copy, scale=gam[:, t0:t1])
+        def close_statistics(t):
+            nc.vector.bn_aggr(out=moments[:, t, :], in_=stats[t][:].rearrange("p n s -> p (n s)"))
+            nc.scalar.activation(out=rstd[:, t : t + 1], in_=moments[:, t, 1:2], func=ACT.Abs_reciprocal_sqrt, bias=EPS)
+            nc.scalar.activation(out=shift[:, t : t + 1], in_=moments[:, t, 0:1], func=ACT.Copy, scale=gam[:, t : t + 1])
 
         def normalise(t, a, b):
-            if (t, a) == (3, S // 2):
-                nc.vector.tensor_scalar(out=z_planes[:, t, a:b], in0=h_copy[t][:, a:b], scalar1=rstd[:, t : t + 1], scalar2=minus_gam[:, 0:1], op0=ALU.mult, op1=ALU.mult)
-                return
-            nc.vector.tensor_scalar(out=z_planes[:, t, a:b], in0=h_copy[t][:, a:b], scalar1=shift[:, t : t + 1], scalar2=rstd[:, t : t + 1], op0=ALU.subtract, op1=ALU.mult)
+            nc.vector.tensor_scalar(
+                out=z_planes[:, t, a:b],
+                in0=h_copy[t][:, a:b],
+                scalar1=shift[:, t : t + 1],
+                scalar2=rstd[:, t : t + 1],
+                op0=ALU.subtract,
+                op1=ALU.mult,
+            )
 
-        def weave_z(on_vector, h, a=0, b=P):
-            dst = z_grouped[h][:, a:b, :].rearrange("p (c i) t -> p c t i", i=4)
-            src = z_planes[:, :, h * P + a : h * P + b].rearrange("p t (c i) -> p c t i", i=4)
-            if on_vector:
-                nc.vector.tensor_copy(out=dst, in_=src)
-            else:
-                nc.scalar.copy(out=dst, in_=src)
+        def join_z(on_vector, c, a, b):
+            interleave(copy_bits, on_vector, z_joined[c][:, a:b, :], z_planes[:, :, c * QUARTER + a : c * QUARTER + b])
 
-        copy_out(0, 1)
-        statistics(0, 0)
-        copy_out(1, 1)
-        statistics(1, 0)
-        statistics(0, 1)
-        copy_out(0, 0)
-        copy_out(1, 0)
-        statistics(1, 1)
-        aggregate(0)
-        inverse_root(0, 1)
-        scaled_mean(0, 1)
+        nc.scalar.activation(out=minus_gam[:], in_=gam[:, LAST : LAST + 1], func=ACT.Copy, scale=-1.0)
+        for t in (0, 1):
+            copy_out(t, 1)
+            statistics(t, 0)
+        for t in (0, 1):
+            statistics(t, 1)
+            copy_out(t, 0)
+        close_statistics(0)
         statistics(2, 0)
-        aggregate(1)
+        close_statistics(1)
         copy_out(2, 0)
-        inverse_root(1, 2)
-        scaled_mean(1, 2)
         statistics(2, 1)
         copy_out(2, 1)
-        statistics(3, 0)
-        aggregate(2)
-        inverse_root(2, 3)
-        scaled_mean(2, 3)
-        copy_out(3, 0)
-        statistics(3, 1)
+        statistics(LAST, 0)
+        close_statistics(2)
+        copy_out(LAST, 0)
+        statistics(LAST, 1)
         normalise(0, 0, S)
-        aggregate(3)
-        inverse_root(3, 4)
-        scaled_mean(3, 4)
-        copy_out(3, 1)
+        close_statistics(LAST)
+        nc.scalar.activation(out=h_copy[LAST][:, HALF:S], in_=banks[LAST, 1][:], func=ACT.Identity, scale=-1.0, bias=moments[:, LAST, 0:1])
         normalise(1, 0, S)
         normalise(2, 0, S)
-        normalise(3, 0, 256)
-        weave_z(False, 1)
-        normalise(3, 256, S)
-        weave_z(True, 0)
-        weave_z(False, 3, 0, 64)
-        weave_z(True, 2)
-        weave_z(True, 3, 64, P)
-        acc_tags = {1: ("h_0_0", "h_0_256"), 2: ("h_2_0", "h_3_0"), 3: ("h_2_256", "h_1_256")}
-        out_rows = out.rearrange("(b p) n -> p b n", p=P)
-        for h in range(4):
-            z_codes = keep.tile([P, P], U32, name=f"z_codes_{h}", align_bytes=64)
-            z_scales = keep.tile([P, P], U8, name=f"z_scales_{h}", align_bytes=64)
-            nc.vector.quantize_mx(out=z_codes[:].bitcast(FP8X4), scales=z_scales[:], in_=z_grouped[h][:].rearrange("p n j -> p (n j)"))
-            result = keep.tile([P, 2, P], F32, name=f"result_{h}")
-            if h == 0:
-                both = psum.tile([P, 2, P], F32, name="acc_0", tag="h_1_0")
-                accs = [both[:, 0, :], both[:, 1, :]]
+        normalise(LAST, 0, HALF)
+        join_z(False, 1, 0, QUARTER)
+        nc.vector.tensor_scalar(
+            out=z_planes[:, LAST, HALF:S],
+            in0=h_copy[LAST][:, HALF:S],
+            scalar1=rstd[:, LAST : LAST + 1],
+            scalar2=minus_gam[:],
+            op0=ALU.mult,
+            op1=ALU.mult,
+        )
+        join_z(True, 0, 0, QUARTER)
+        join_z(False, 3, 0, QUARTER // 2)
+        join_z(True, 2, 0, QUARTER)
+        join_z(True, 3, QUARTER // 2, QUARTER)
+
+        banks_of = {1: ("h_0_0", "h_0_1"), 2: ("h_2_0", "h_3_0"), 3: ("h_2_1", "h_1_1")}
+        out_rows = out.rearrange("(r p) n -> p r n", p=P)
+        for c in range(4):
+            z_codes = keep.tile([P, QUARTER], U32, name=f"z_codes_{c}", align_bytes=ALIGN)
+            z_scales = keep.tile([P, QUARTER], U8, name=f"z_scales_{c}", align_bytes=ALIGN)
+            nc.vector.quantize_mx(out=z_codes[:].bitcast(FP8X4), scales=z_scales[:], in_=z_joined[c][:].rearrange("p n t -> p (n t)"))
+            result = keep.tile([P, 2, QUARTER], F32, name=f"result_{c}")
+            if c == 0:
+                shared = psum.tile([P, 2, QUARTER], F32, name="acc_0", tag="h_1_0")
+                sums = [shared[:, r, :] for r in range(2)]
             else:
-                accs = [psum.tile([P, P], F32, name=f"acc_{h}_{b}", tag=acc_tags[h][b])[:] for b in range(2)]
-            for b in range(2):
+                sums = [psum.tile([P, QUARTER], F32, name=f"acc_{c}_{r}", tag=banks_of[c][r])[:] for r in range(2)]
+            for r in range(2):
                 nc.tensor.matmul_mx(
-                    out=accs[b],
-                    lhsT=w2_codes[:, b * P : (b + 1) * P].bitcast(FP8X4),
-                    lhsT_scale=w2_plane[:, b * P : (b + 1) * P],
+                    out=sums[r],
+                    lhsT=w2_codes[:, r * P : (r + 1) * P].bitcast(FP8X4),
+                    lhsT_scale=w2_plane[:, r * P : (r + 1) * P],
                     rhs=z_codes[:].bitcast(FP8X4),
                     rhs_scale=z_scales[:],
                     start=True,
                     stop=True,
                 )
-            if h == 0:
-                cast(False, result[:], both[:])
+            if c == 0:
+                copy_floats(False, result[:], shared[:])
             else:
-                for b in range(2):
-                    cast(b == 1, result[:, b, :], accs[b])
-            nc.sync.dma_start(out=out_rows[:, :, h * P : (h + 1) * P], in_=result[:])
+                for r in range(2):
+                    copy_floats(r == 1, result[:, r, :], sums[r])
+            nc.sync.dma_start(out=out_rows[:, :, c * QUARTER : (c + 1) * QUARTER], in_=result[:])

@@ -25,7 +25,7 @@ LAST = PACK - 1
 EPS = 1e-5
 ALIGN = 64
 
-X_ON_VECTOR = ((688, 688), (656, 480))
+X_ON_VECTOR = ((688, 656), (672, 432))
 W_ON_SCALAR = ((P, P), (64, 48))
 
 
@@ -205,8 +205,8 @@ def tile_picked_inorm_none_e_kernel(tc, xT, w1, w2_words, w2_scales, gamma, offs
                 op1=ALU.mult,
             )
 
-        def join_z(on_vector, c, a, b):
-            interleave(copy_bits, on_vector, z_joined[c][:, a:b, :], z_planes[:, :, c * QUARTER + a : c * QUARTER + b])
+        def join_z(on_vector, c):
+            interleave(copy_bits, on_vector, z_joined[c][:], z_planes[:, :, c * QUARTER : (c + 1) * QUARTER])
 
         nc.scalar.activation(out=minus_gam[:], in_=gam[:, LAST : LAST + 1], func=ACT.Copy, scale=-1.0)
         for t in (0, 1):
@@ -231,7 +231,7 @@ def tile_picked_inorm_none_e_kernel(tc, xT, w1, w2_words, w2_scales, gamma, offs
         normalise(1, 0, S)
         normalise(2, 0, S)
         normalise(LAST, 0, HALF)
-        join_z(False, 1, 0, QUARTER)
+        join_z(False, 1)
         nc.vector.tensor_scalar(
             out=z_planes[:, LAST, HALF:S],
             in0=h_copy[LAST][:, HALF:S],
@@ -240,18 +240,19 @@ def tile_picked_inorm_none_e_kernel(tc, xT, w1, w2_words, w2_scales, gamma, offs
             op0=ALU.mult,
             op1=ALU.mult,
         )
-        join_z(True, 0, 0, QUARTER)
-        join_z(False, 3, 0, QUARTER // 2)
-        join_z(True, 2, 0, QUARTER)
-        join_z(True, 3, QUARTER // 2, QUARTER)
+        join_z(True, 0)
+        join_z(False, 3)
+        join_z(True, 2)
 
         banks_of = {1: ("h_0_0", "h_0_1"), 2: ("h_2_0", "h_3_0"), 3: ("h_2_1", "h_1_1")}
         out_rows = out.rearrange("(r p) n -> p r n", p=P)
+        result = keep.tile([P, 2, S], F32, name="result")
+        stores = {0: (0, QUARTER), 2: (QUARTER, 3 * QUARTER), 3: (3 * QUARTER, S)}
         for c in range(4):
+            cols = slice(c * QUARTER, (c + 1) * QUARTER)
             z_codes = keep.tile([P, QUARTER], U32, name=f"z_codes_{c}", align_bytes=ALIGN)
             z_scales = keep.tile([P, QUARTER], U8, name=f"z_scales_{c}", align_bytes=ALIGN)
             nc.vector.quantize_mx(out=z_codes[:].bitcast(FP8X4), scales=z_scales[:], in_=z_joined[c][:].rearrange("p n t -> p (n t)"))
-            result = keep.tile([P, 2, QUARTER], F32, name=f"result_{c}")
             if c == 0:
                 shared = psum.tile([P, 2, QUARTER], F32, name="acc_0", tag="h_1_0")
                 sums = [shared[:, r, :] for r in range(2)]
@@ -268,8 +269,10 @@ def tile_picked_inorm_none_e_kernel(tc, xT, w1, w2_words, w2_scales, gamma, offs
                     stop=True,
                 )
             if c == 0:
-                copy_floats(False, result[:], shared[:])
+                copy_floats(False, result[:, :, cols], shared[:])
             else:
                 for r in range(2):
-                    copy_floats(r == 1, result[:, r, :], sums[r])
-            nc.sync.dma_start(out=out_rows[:, :, c * QUARTER : (c + 1) * QUARTER], in_=result[:])
+                    copy_floats(r == 1, result[:, r, cols], sums[r])
+            if c in stores:
+                a, b = stores[c]
+                nc.sync.dma_start(out=out_rows[:, :, a:b], in_=result[:, :, a:b])

@@ -52,14 +52,15 @@ def tile_picked_inorm_none_e_kernel(tc, xT, w1, w2_words, w2_scales, gamma, offs
         psum = ctx.enter_context(tc.psum_pool(name="psum", bufs=1))
 
         offsets = keep.tile([P, S // 16], U16, name="offsets")
-        w2_codes = keep.tile([P, N], U32, name="w2_codes", align_bytes=ALIGN)
         w2_plane = keep.tile([P, N], U8, name="w2_plane", align_bytes=ALIGN)
-        gam = keep.tile([P, PACK], F32, name="gam")
         preload = keep.tile([P, 2], F32, name="preload")
 
-        nc.vector.memset(w2_plane[:].bitcast(U32), 0)
+        nc.gpsimd.memset(w2_plane[:].bitcast(U32), 0)
         nc.vector.memset(preload[:, 0:1], 1.0)
         nc.scalar.activation(out=preload[:, 1:2], in_=preload[:, 0:1], func=ACT.Abs_reciprocal_sqrt)
+
+        def load_scale_rows(q):
+            nc.sync.dma_start(out=w2_plane[32 * q : 32 * q + 4, :].bitcast(I32), in_=w2_scales[0, 4 * q : 4 * q + 4, :].bitcast(I32))
 
         x_raw = {}
         for g in range(PASSES):
@@ -69,14 +70,16 @@ def tile_picked_inorm_none_e_kernel(tc, xT, w1, w2_words, w2_scales, gamma, offs
                 nc.sync.dma_start(out=x_raw[g, u][:], in_=rows[:, 2 * u : 2 * u + 2, :])
                 if (g, u) == (0, 0):
                     nc.sync.dma_start(offsets[:], offs)
+                    for q in range(3):
+                        load_scale_rows(q)
         w_raw = {}
-        for g in range(PASSES):
-            w_raw[g] = keep.tile([P, PACK, H], F32, name=f"w_raw_{g}", align_bytes=ALIGN)
+
+        def load_weights(g, tag):
+            w_raw[g] = keep.tile([P, PACK, H], F32, name=f"w_raw_{g}", tag=tag, align_bytes=ALIGN)
             nc.sync.dma_start(out=w_raw[g][:], in_=w1[g * K_PASS : (g + 1) * K_PASS, :].rearrange("(p j) n -> p j n", j=PACK))
-        nc.sync.dma_start(out=gam[:], in_=gamma.rearrange("(p t) o -> p (t o)", t=PACK))
-        nc.sync.dma_start(out=w2_codes[:].bitcast(I32), in_=w2_words[0].rearrange("p n j -> p (n j)").bitcast(I32))
-        for q in range(4):
-            nc.sync.dma_start(out=w2_plane[32 * q : 32 * q + 4, :].bitcast(I32), in_=w2_scales[0, 4 * q : 4 * q + 4, :].bitcast(I32))
+
+        load_weights(0, "w_raw_0")
+        load_scale_rows(3)
 
         found = [keep.tile([P, 2, S], U32, name=f"x_found_{g}", align_bytes=ALIGN) for g in range(PASSES)]
         joined = {}
@@ -98,9 +101,16 @@ def tile_picked_inorm_none_e_kernel(tc, xT, w1, w2_words, w2_scales, gamma, offs
             for n in range(2):
                 interleave(copy_bits, on_vector, joined[g][:, n].bitcast(view), found[g][:, :, n * HALF : (n + 1) * HALF].bitcast(view))
 
+        first_codes = keep.tile([P, S], U32, name="x_codes_0", align_bytes=ALIGN)
+        first_scales = keep.tile([P, S], U8, name="x_scales_0", align_bytes=ALIGN)
+
         def quantise_points(g, n, tag):
-            x_codes[g, n] = keep.tile([P, HALF], U32, name=f"x_codes_{g}_{n}", tag=tag, align_bytes=ALIGN)
-            x_scales[g, n] = keep.tile([P, HALF], U8, name=f"x_scales_{g}_{n}", align_bytes=ALIGN)
+            if g == 0:
+                x_codes[g, n] = first_codes[:, n * HALF : (n + 1) * HALF]
+                x_scales[g, n] = first_scales[:, n * HALF : (n + 1) * HALF]
+            else:
+                x_codes[g, n] = keep.tile([P, HALF], U32, name=f"x_codes_{g}_{n}", tag=tag, align_bytes=ALIGN)
+                x_scales[g, n] = keep.tile([P, HALF], U8, name=f"x_scales_{g}_{n}", align_bytes=ALIGN)
             nc.vector.quantize_mx(
                 out=x_codes[g, n][:].bitcast(FP8X4),
                 scales=x_scales[g, n][:],
@@ -135,7 +145,12 @@ def tile_picked_inorm_none_e_kernel(tc, xT, w1, w2_words, w2_scales, gamma, offs
 
         whole_list = [(0, S)]
         look_up(0, 0, whole_list)
+        load_weights(1, "x_raw_0_0")
         look_up(0, 1, whole_list)
+        gam = keep.tile([P, PACK], F32, name="gam", tag="x_pairs_0_0", align_bytes=ALIGN)
+        nc.sync.dma_start(out=gam[:], in_=gamma.rearrange("(p t) o -> p (t o)", t=PACK))
+        w2_codes = keep.tile([P, N], U32, name="w2_codes", tag="x_raw_0_1", align_bytes=ALIGN)
+        nc.sync.dma_start(out=w2_codes[:].bitcast(I32), in_=w2_words[0].rearrange("p n j -> p (n j)").bitcast(I32))
         look_up(1, 0, whole_list)
         join(0, False, "x_raw_1_0")
         quantise_points(0, 0, "x_codes_0_0")
@@ -151,7 +166,19 @@ def tile_picked_inorm_none_e_kernel(tc, xT, w1, w2_words, w2_scales, gamma, offs
         quantise_points(1, 1, "w_dealt_0_0")
         quantise_weights(1, 0, [(0, 1), (1, 2)], "w_codes_1_0")
         quantise_weights(1, 1, both_tiles, "w_codes_1_1")
-        quantise_weights(0, 1, both_tiles, "w_raw_1")
+        quantise_weights(0, 1, both_tiles, "x_raw_0_0")
+
+        idle = psum.tile([P, S], F32, name="idle", tag="h_3_1")
+        for r in range(2):
+            nc.tensor.matmul_mx(
+                out=idle[:],
+                lhsT=first_codes[:, r * P : (r + 1) * P].bitcast(FP8X4),
+                lhsT_scale=w2_plane[:, r * P : (r + 1) * P],
+                rhs=first_codes[:].bitcast(FP8X4),
+                rhs_scale=first_scales[:],
+                start=True,
+                stop=True,
+            )
 
         banks = {(t, n): psum.tile([P, HALF], F32, name=f"h_{t}_{n}") for t in range(PACK) for n in range(2)}
 

@@ -24,9 +24,11 @@ QUARTER = S // 4
 LAST = PACK - 1
 EPS = 1e-5
 ALIGN = 64
+LAST_JOIN_ON_SCALAR = 48
+NARROW = 32
 
-X_ON_VECTOR = ((688, 656), (672, 432))
-W_ON_SCALAR = ((P, P), (64, 48))
+JOIN_ON_VECTOR = (256, 352)
+W_ON_SCALAR = ((44, 96), (44, 52))
 
 
 def tile_picked_inorm_none_e_kernel(tc, xT, w1, w2_words, w2_scales, gamma, offs, out):
@@ -44,8 +46,8 @@ def tile_picked_inorm_none_e_kernel(tc, xT, w1, w2_words, w2_scales, gamma, offs
         else:
             nc.scalar.copy(out=dst, in_=src)
 
-    def interleave(copy, on_vector, dst, src):
-        copy(on_vector, dst.rearrange("p (c i) r -> p c r i", i=4), src.rearrange("p r (c i) -> p c r i", i=4))
+    def interleave(copy, on_vector, dst, src, i=4):
+        copy(on_vector, dst.rearrange("p (c i) r -> p c r i", i=i), src.rearrange("p r (c i) -> p c r i", i=i))
 
     with ExitStack() as ctx:
         keep = ctx.enter_context(tc.tile_pool(name="keep", bufs=1))
@@ -54,10 +56,13 @@ def tile_picked_inorm_none_e_kernel(tc, xT, w1, w2_words, w2_scales, gamma, offs
         offsets = keep.tile([P, S // 16], U16, name="offsets")
         w2_plane = keep.tile([P, N], U8, name="w2_plane", align_bytes=ALIGN)
         preload = keep.tile([P, 2], F32, name="preload")
+        moments = keep.tile([P, PACK, 4], F32, name="moments")
 
         nc.gpsimd.memset(w2_plane[:].bitcast(U32), 0)
         nc.vector.memset(preload[:, 0:1], 1.0)
         nc.scalar.activation(out=preload[:, 1:2], in_=preload[:, 0:1], func=ACT.Abs_reciprocal_sqrt)
+        nc.vector.memset(moments[:, :, 0:1], -1.0)
+        nc.vector.memset(moments[:, 1, 0:1], -float(S))
 
         def load_scale_rows(q):
             nc.sync.dma_start(out=w2_plane[32 * q : 32 * q + 4, :].bitcast(I32), in_=w2_scales[0, 4 * q : 4 * q + 4, :].bitcast(I32))
@@ -70,52 +75,49 @@ def tile_picked_inorm_none_e_kernel(tc, xT, w1, w2_words, w2_scales, gamma, offs
                 nc.sync.dma_start(out=x_raw[g, u][:], in_=rows[:, 2 * u : 2 * u + 2, :])
                 if (g, u) == (0, 0):
                     nc.sync.dma_start(offsets[:], offs)
-                    for q in range(3):
-                        load_scale_rows(q)
         w_raw = {}
-
-        def load_weights(g, tag):
-            w_raw[g] = keep.tile([P, PACK, H], F32, name=f"w_raw_{g}", tag=tag, align_bytes=ALIGN)
+        for g in range(PASSES):
+            w_raw[g] = keep.tile([P, PACK, H], F32, name=f"w_raw_{g}", align_bytes=ALIGN)
             nc.sync.dma_start(out=w_raw[g][:], in_=w1[g * K_PASS : (g + 1) * K_PASS, :].rearrange("(p j) n -> p j n", j=PACK))
+            if g == 0:
+                load_scale_rows(0)
+        gam = keep.tile([P, PACK], F32, name="gam", align_bytes=ALIGN)
+        nc.sync.dma_start(out=gam[:], in_=gamma.rearrange("(p t) o -> p (t o)", t=PACK))
+        w2_codes = keep.tile([P, N], U32, name="w2_codes", align_bytes=ALIGN)
+        nc.sync.dma_start(out=w2_codes[:].bitcast(I32), in_=w2_words[0].rearrange("p n j -> p (n j)").bitcast(I32))
 
-        load_weights(0, "w_raw_0")
-        load_scale_rows(3)
-
-        found = [keep.tile([P, 2, S], U32, name=f"x_found_{g}", align_bytes=ALIGN) for g in range(PASSES)]
-        joined = {}
-        x_codes = {}
-        x_scales = {}
-
-        def look_up(g, u, spans):
-            cut = X_ON_VECTOR[g][u]
-            pairs = keep.tile([P, T], U32, name=f"x_pairs_{g}_{u}", align_bytes=ALIGN)
-            values = pairs[:].bitcast(BF16).rearrange("p (n j) -> p n j", j=2)
-            interleave(copy_floats, False, values[:, cut:T, :], x_raw[g, u][:, :, cut:T])
-            interleave(copy_floats, True, values[:, 0:cut, :], x_raw[g, u][:, :, 0:cut])
-            for a, b in spans:
-                nc.vector.tensor_copy(out=found[g][:, u, a:b], in_=pairs[:].indirect(offsets[:, a // 16 : b // 16]))
-
-        def join(g, on_vector, tag):
-            joined[g] = keep.tile([P, 2, HALF, 2], U32, name=f"x_joined_{g}", tag=tag, align_bytes=ALIGN)
-            view = I32 if on_vector else U32
-            for n in range(2):
-                interleave(copy_bits, on_vector, joined[g][:, n].bitcast(view), found[g][:, :, n * HALF : (n + 1) * HALF].bitcast(view))
-
+        joined = [keep.tile([P, S, PACK], BF16, name=f"x_joined_{g}", align_bytes=ALIGN) for g in range(PASSES)]
         first_codes = keep.tile([P, S], U32, name="x_codes_0", align_bytes=ALIGN)
         first_scales = keep.tile([P, S], U8, name="x_scales_0", align_bytes=ALIGN)
+        late_codes = {}
+        late_scales = {}
 
         def quantise_points(g, n, tag):
+            cols = slice(n * HALF, (n + 1) * HALF)
             if g == 0:
-                x_codes[g, n] = first_codes[:, n * HALF : (n + 1) * HALF]
-                x_scales[g, n] = first_scales[:, n * HALF : (n + 1) * HALF]
+                codes, plane = first_codes[:, cols], first_scales[:, cols]
             else:
-                x_codes[g, n] = keep.tile([P, HALF], U32, name=f"x_codes_{g}_{n}", tag=tag, align_bytes=ALIGN)
-                x_scales[g, n] = keep.tile([P, HALF], U8, name=f"x_scales_{g}_{n}", align_bytes=ALIGN)
-            nc.vector.quantize_mx(
-                out=x_codes[g, n][:].bitcast(FP8X4),
-                scales=x_scales[g, n][:],
-                in_=joined[g][:, n].rearrange("p n u -> p (n u)").bitcast(BF16),
-            )
+                late_codes[n] = keep.tile([P, HALF], U32, name=f"x_codes_1_{n}", tag=tag, align_bytes=ALIGN)
+                late_scales[n] = keep.tile([P, HALF], U8, name=f"x_scales_1_{n}", align_bytes=ALIGN)
+                codes, plane = late_codes[n][:], late_scales[n][:]
+            nc.vector.quantize_mx(out=codes.bitcast(FP8X4), scales=plane, in_=joined[g][:, cols, :].rearrange("p n j -> p (n j)"))
+
+        found = {}
+        for g in range(PASSES):
+            found[g] = keep.tile([P, PACK, S], F32, name=f"x_found_{g}", align_bytes=ALIGN)
+            for u in range(2):
+                for a, b in [(0, HALF), (HALF, S)] if (g, u) == (1, 1) else [(0, S)]:
+                    part = offsets[:, a // 16 : b // 16]
+                    nc.vector.tensor_copy(out=found[g][:, 2 * u, a:b], in_=x_raw[g, u][:, 0, :].indirect(part))
+                    nc.scalar.activation(out=found[g][:, 2 * u + 1, a:b], in_=x_raw[g, u][:, 1, :].indirect(part), func=ACT.Copy)
+            cut = JOIN_ON_VECTOR[g]
+            interleave(copy_floats, True, joined[g][:, 0:HALF, :], found[g][:, :, 0:HALF])
+            if cut > HALF:
+                interleave(copy_floats, True, joined[g][:, HALF:cut, :], found[g][:, :, HALF:cut])
+            interleave(copy_floats, False, joined[g][:, cut:S, :], found[g][:, :, cut:S])
+            if g == 0:
+                for n in range(2):
+                    quantise_points(0, n, None)
 
         dealt = {}
         w_codes = {}
@@ -126,162 +128,153 @@ def tile_picked_inorm_none_e_kernel(tc, xT, w1, w2_words, w2_scales, gamma, offs
             dealt[g, u] = keep.tile([P, 2, P, PACK], BF16, name=f"w_dealt_{g}_{u}", align_bytes=ALIGN)
             dst = dealt[g, u][:].rearrange("p s m j -> p m j s")
             src = w_raw[g][:].rearrange("p j (m t) -> p m j t", t=PACK)[:, :, :, 2 * u : 2 * u + 2]
-            copy_floats(False, dst[:, 0:cut], src[:, 0:cut])
+            if cut > 0:
+                copy_floats(False, dst[:, 0:cut], src[:, 0:cut])
             if cut < P:
                 copy_floats(True, dst[:, cut:P], src[:, cut:P])
 
-        def quantise_weights(g, u, spans, tag):
-            codes = keep.tile([P, 2 * P], U32, name=f"w_codes_{g}_{u}", tag=tag, align_bytes=ALIGN)
-            plane = keep.tile([P, 2 * P], U8, name=f"w_scales_{g}_{u}", align_bytes=ALIGN)
+        def quantise_weights(g, u, spans):
             for s0, s1 in spans:
+                codes = keep.tile([P, (s1 - s0) * P], U32, name=f"w_codes_{g}_{u}_{s0}", align_bytes=ALIGN)
+                plane = keep.tile([P, (s1 - s0) * P], U8, name=f"w_scales_{g}_{u}_{s0}", align_bytes=ALIGN)
                 nc.vector.quantize_mx(
-                    out=codes[:, s0 * P : s1 * P].bitcast(FP8X4),
-                    scales=plane[:, s0 * P : s1 * P],
+                    out=codes[:].bitcast(FP8X4),
+                    scales=plane[:],
                     in_=dealt[g, u][:, s0:s1].rearrange("p s m j -> p (s m j)"),
                 )
-            for s in range(2):
-                w_codes[g, 2 * u + s] = codes[:, s * P : (s + 1) * P]
-                w_scales[g, 2 * u + s] = plane[:, s * P : (s + 1) * P]
+                for s in range(s0, s1):
+                    w_codes[g, 2 * u + s] = codes[:, (s - s0) * P : (s - s0 + 1) * P]
+                    w_scales[g, 2 * u + s] = plane[:, (s - s0) * P : (s - s0 + 1) * P]
 
-        whole_list = [(0, S)]
-        look_up(0, 0, whole_list)
-        load_weights(1, "x_raw_0_0")
-        look_up(0, 1, whole_list)
-        gam = keep.tile([P, PACK], F32, name="gam", tag="x_pairs_0_0", align_bytes=ALIGN)
-        nc.sync.dma_start(out=gam[:], in_=gamma.rearrange("(p t) o -> p (t o)", t=PACK))
-        w2_codes = keep.tile([P, N], U32, name="w2_codes", tag="x_raw_0_1", align_bytes=ALIGN)
-        nc.sync.dma_start(out=w2_codes[:].bitcast(I32), in_=w2_words[0].rearrange("p n j -> p (n j)").bitcast(I32))
-        look_up(1, 0, whole_list)
-        join(0, False, "x_raw_1_0")
-        quantise_points(0, 0, "x_codes_0_0")
-        quantise_points(0, 1, "x_codes_0_1")
-        look_up(1, 1, [(0, HALF), (HALF, S)])
-        join(1, True, "x_joined_1")
         quantise_points(1, 0, "x_codes_1_0")
-        for g in range(PASSES):
-            for u in range(2):
-                deal_weights(g, u)
-        both_tiles = [(0, 2)]
-        quantise_weights(0, 0, both_tiles, "w_codes_0_0")
+        deal_weights(0, 0)
+        quantise_weights(0, 0, [(0, 2)])
+        deal_weights(0, 1)
         quantise_points(1, 1, "w_dealt_0_0")
-        quantise_weights(1, 0, [(0, 1), (1, 2)], "w_codes_1_0")
-        quantise_weights(1, 1, both_tiles, "w_codes_1_1")
-        quantise_weights(0, 1, both_tiles, "x_raw_0_0")
+        quantise_weights(0, 1, [(0, 2)])
+        for u in range(2):
+            deal_weights(1, u)
+        quantise_weights(1, 0, [(0, 1), (1, 2)])
+        quantise_weights(1, 1, [(0, 1), (1, 2)])
 
-        idle = psum.tile([P, S], F32, name="idle", tag="h_3_1")
-        for r in range(2):
-            nc.tensor.matmul_mx(
-                out=idle[:],
-                lhsT=first_codes[:, r * P : (r + 1) * P].bitcast(FP8X4),
-                lhsT_scale=w2_plane[:, r * P : (r + 1) * P],
-                rhs=first_codes[:].bitcast(FP8X4),
-                rhs_scale=first_scales[:],
-                start=True,
-                stop=True,
-            )
+        spans = {t: [(0, S)] for t in range(LAST)}
+        spans[0] = spans[2] = spans[LAST] = [(0, HALF), (HALF, S)]
 
-        banks = {(t, n): psum.tile([P, HALF], F32, name=f"h_{t}_{n}") for t in range(PACK) for n in range(2)}
+        def warm_up(tag, codes, plane):
+            idle = psum.tile([NARROW, S], F32, name="idle_" + tag, tag=tag)
+            for r in range(2):
+                nc.tensor.matmul_mx(
+                    out=idle[:],
+                    lhsT=codes[:, r * P : r * P + NARROW].bitcast(FP8X4),
+                    lhsT_scale=plane[:, r * P : r * P + NARROW],
+                    rhs=first_codes[:].bitcast(FP8X4),
+                    rhs_scale=first_scales[:],
+                    start=True,
+                    stop=True,
+                )
 
-        def first_product(g, t, n, opens):
-            nc.tensor.matmul_mx(
-                out=banks[t, n][:],
-                lhsT=w_codes[g, t].bitcast(FP8X4),
-                lhsT_scale=w_scales[g, t],
-                rhs=x_codes[g, n][:].bitcast(FP8X4),
-                rhs_scale=x_scales[g, n][:],
-                start=opens,
-                stop=not opens,
-            )
-
-        for g in range(PASSES):
-            for t in (0, 1):
-                for n in range(2):
-                    first_product(g, t, n, g == 0)
-        for t in (2, 3):
+        warm_up("acc_0", first_codes, w2_plane)
+        for q in range(1, 4):
+            load_scale_rows(q)
+        banks = {(t, a): psum.tile([P, b - a], F32, name=f"h_{t}_{a}") for t in range(PACK) for a, b in spans[t]}
+        for t in range(PACK):
+            for a, b in spans[t]:
+                nc.tensor.matmul_mx(
+                    out=banks[t, a][:],
+                    lhsT=w_codes[0, t].bitcast(FP8X4),
+                    lhsT_scale=w_scales[0, t],
+                    rhs=first_codes[:, a:b].bitcast(FP8X4),
+                    rhs_scale=first_scales[:, a:b],
+                    start=True,
+                    stop=False,
+                )
+        for t in range(PACK):
             for n in range(2):
-                for g in (1, 0):
-                    first_product(g, t, n, g == 1)
+                split = len(spans[t]) == 2
+                nc.tensor.matmul_mx(
+                    out=banks[t, n * HALF][:] if split else banks[t, 0][:, n * HALF : (n + 1) * HALF],
+                    lhsT=w_codes[1, t].bitcast(FP8X4),
+                    lhsT_scale=w_scales[1, t],
+                    rhs=late_codes[n][:].bitcast(FP8X4),
+                    rhs_scale=late_scales[n][:],
+                    start=False,
+                    stop=split or n == 1,
+                )
 
-        stats = [keep.tile([P, 2, 6], F32, name=f"stats_{t}") for t in range(PACK)]
-        moments = keep.tile([P, PACK, 2], F32, name="moments")
+        stats = [keep.tile([P, len(spans[t]), 6], F32, name=f"stats_{t}") for t in range(PACK)]
         rstd = keep.tile([P, PACK], F32, name="rstd")
-        shift = keep.tile([P, PACK], F32, name="shift")
-        minus_gam = keep.tile([P, 1], F32, name="minus_gam")
-        h_copy = [keep.tile([P, S], F32, name=f"h_copy_{t}") for t in range(PACK)]
+        factors = [keep.tile([P, 2], F32, name=f"factors_{t}") for t in range(PACK)]
+        minus_gam = keep.tile([P, PACK], F32, name="minus_gam")
+        h_copy = keep.tile([P, S], F32, name="h_copy")
         z_planes = keep.tile([P, PACK, S], BF16, name="z_planes", align_bytes=ALIGN)
         z_joined = [keep.tile([P, QUARTER, PACK], BF16, name=f"z_joined_{c}", align_bytes=ALIGN) for c in range(4)]
+        nc.scalar.activation(out=minus_gam[:], in_=gam[:], func=ACT.Copy, scale=-1.0)
 
-        def statistics(t, n):
-            nc.vector.bn_stats(out=stats[t][:, n, :], in_=banks[t, n][:])
-
-        def copy_out(t, n):
-            nc.scalar.activation(out=h_copy[t][:, n * HALF : (n + 1) * HALF], in_=banks[t, n][:], func=ACT.Copy, scale=gam[:, t : t + 1])
-
-        def close_statistics(t):
-            nc.vector.bn_aggr(out=moments[:, t, :], in_=stats[t][:].rearrange("p n s -> p (n s)"))
-            nc.scalar.activation(out=rstd[:, t : t + 1], in_=moments[:, t, 1:2], func=ACT.Abs_reciprocal_sqrt, bias=EPS)
-            nc.scalar.activation(out=shift[:, t : t + 1], in_=moments[:, t, 0:1], func=ACT.Copy, scale=gam[:, t : t + 1])
-
-        def normalise(t, a, b):
-            nc.vector.tensor_scalar(
-                out=z_planes[:, t, a:b],
-                in0=h_copy[t][:, a:b],
-                scalar1=shift[:, t : t + 1],
-                scalar2=rstd[:, t : t + 1],
-                op0=ALU.subtract,
-                op1=ALU.mult,
+        def make_factors(engine, t, signed_gam):
+            engine.tensor_scalar(
+                out=factors[t][:], in0=moments[:, t, 0:2], scalar1=rstd[:, t : t + 1], scalar2=signed_gam[:, t : t + 1], op0=ALU.mult, op1=ALU.mult
             )
 
-        def join_z(on_vector, c):
-            interleave(copy_bits, on_vector, z_joined[c][:], z_planes[:, :, c * QUARTER : (c + 1) * QUARTER])
+        def close(t):
+            nc.vector.bn_aggr(out=moments[:, t, 1:3], in_=stats[t][:].rearrange("p n s -> p (n s)"))
+            nc.scalar.activation(out=rstd[:, t : t + 1], in_=moments[:, t, 2:3], func=ACT.Abs_reciprocal_sqrt, bias=EPS)
 
-        nc.scalar.activation(out=minus_gam[:], in_=gam[:, LAST : LAST + 1], func=ACT.Copy, scale=-1.0)
-        for t in (0, 1):
-            copy_out(t, 1)
-            statistics(t, 0)
-        for t in (0, 1):
-            statistics(t, 1)
-            copy_out(t, 0)
-        close_statistics(0)
-        statistics(2, 0)
-        close_statistics(1)
-        copy_out(2, 0)
-        statistics(2, 1)
-        copy_out(2, 1)
-        statistics(LAST, 0)
-        close_statistics(2)
-        copy_out(LAST, 0)
-        statistics(LAST, 1)
-        normalise(0, 0, S)
-        close_statistics(LAST)
-        nc.scalar.activation(out=h_copy[LAST][:, HALF:S], in_=banks[LAST, 1][:], func=ACT.Identity, scale=-1.0, bias=moments[:, LAST, 0:1])
-        normalise(1, 0, S)
-        normalise(2, 0, S)
-        normalise(LAST, 0, HALF)
-        join_z(False, 1)
-        nc.vector.tensor_scalar(
-            out=z_planes[:, LAST, HALF:S],
-            in0=h_copy[LAST][:, HALF:S],
-            scalar1=rstd[:, LAST : LAST + 1],
-            scalar2=minus_gam[:],
-            op0=ALU.mult,
-            op1=ALU.mult,
-        )
-        join_z(True, 0)
-        join_z(False, 3)
-        join_z(True, 2)
+        def normalise(on_vector, t, a, b, src):
+            if on_vector:
+                nc.vector.tensor_scalar(
+                    out=z_planes[:, t, a:b], in0=src, scalar1=factors[t][:, 0:1], scalar2=factors[t][:, 1:2], op0=ALU.mult, op1=ALU.add
+                )
+            else:
+                nc.scalar.activation(out=z_planes[:, t, a:b], in_=src, func=ACT.Identity, scale=factors[t][:, 0:1], bias=factors[t][:, 1:2])
 
-        banks_of = {1: ("h_0_0", "h_0_1"), 2: ("h_2_0", "h_3_0"), 3: ("h_2_1", "h_1_1")}
+        def part_statistics(t, n):
+            if len(spans[t]) == 1:
+                nc.vector.bn_stats(out=stats[t][:, n, :], in_=banks[t, 0][:, n * HALF : (n + 1) * HALF])
+            else:
+                nc.vector.bn_stats(out=stats[t][:, n, :], in_=banks[t, n * HALF][:])
+
+        part_statistics(0, 0)
+        part_statistics(0, 1)
+        nc.scalar.activation(out=h_copy[:], in_=banks[1, 0][:], func=ACT.Copy, scale=-1.0 / S, accum_out=moments[:, 1, 1:2])
+        part_statistics(2, 0)
+        close(0)
+        part_statistics(2, 1)
+        nc.scalar.activation(out=z_planes[:, 1, :], in_=banks[1, 0][:], func=ACT.Square, bias=moments[:, 1, 1:2], accum_out=moments[:, 1, 2:3])
+        part_statistics(LAST, 0)
+        make_factors(nc.vector, 0, minus_gam)
+        close(2)
+        part_statistics(LAST, 1)
+        nc.scalar.activation(out=rstd[:, 1:2], in_=moments[:, 1, 2:3], func=ACT.Abs_reciprocal_sqrt, scale=1.0 / S, bias=EPS)
+        make_factors(nc.vector, 2, minus_gam)
+        normalise(False, 0, 0, HALF, banks[0, 0][:])
+        warm_up("h_0_0", late_codes[0], late_scales[0])
+        close(LAST)
+        make_factors(nc.vector, 1, gam)
+        normalise(False, 0, HALF, S, banks[0, HALF][:])
+        normalise(True, 2, 0, HALF, banks[2, 0][:])
+        make_factors(nc.vector, LAST, minus_gam)
+        normalise(True, 1, 0, S, h_copy[:])
+        normalise(False, 2, HALF, S, banks[2, HALF][:])
+        normalise(True, LAST, 0, QUARTER, banks[LAST, 0][:, 0:QUARTER])
+        normalise(True, LAST, QUARTER, HALF, banks[LAST, 0][:, QUARTER:HALF])
+        normalise(False, LAST, HALF, S, banks[LAST, HALF][:])
+
+
+        def join_z(on_vector, c, a, b):
+            interleave(copy_bits, on_vector, z_joined[c][:, a:b, :], z_planes[:, :, c * QUARTER + a : c * QUARTER + b])
+
+        banks_of = {1: ("h_1_0", "h_0_0"), 2: ("h_2_0", "h_0_256"), 3: ("h_2_256", "h_3_0")}
         out_rows = out.rearrange("(r p) n -> p r n", p=P)
         result = keep.tile([P, 2, S], F32, name="result")
         stores = {0: (0, QUARTER), 2: (QUARTER, 3 * QUARTER), 3: (3 * QUARTER, S)}
-        for c in range(4):
+        z_codes = [keep.tile([P, QUARTER], U32, name=f"z_codes_{c}", align_bytes=ALIGN) for c in range(4)]
+
+        def second_product(c):
             cols = slice(c * QUARTER, (c + 1) * QUARTER)
-            z_codes = keep.tile([P, QUARTER], U32, name=f"z_codes_{c}", align_bytes=ALIGN)
             z_scales = keep.tile([P, QUARTER], U8, name=f"z_scales_{c}", align_bytes=ALIGN)
-            nc.vector.quantize_mx(out=z_codes[:].bitcast(FP8X4), scales=z_scales[:], in_=z_joined[c][:].rearrange("p n t -> p (n t)"))
+            nc.vector.quantize_mx(out=z_codes[c][:].bitcast(FP8X4), scales=z_scales[:], in_=z_joined[c][:].rearrange("p n t -> p (n t)"))
             if c == 0:
-                shared = psum.tile([P, 2, QUARTER], F32, name="acc_0", tag="h_1_0")
+                shared = psum.tile([P, 2, QUARTER], F32, name="acc_0")
                 sums = [shared[:, r, :] for r in range(2)]
             else:
                 sums = [psum.tile([P, QUARTER], F32, name=f"acc_{c}_{r}", tag=banks_of[c][r])[:] for r in range(2)]
@@ -290,7 +283,7 @@ def tile_picked_inorm_none_e_kernel(tc, xT, w1, w2_words, w2_scales, gamma, offs
                     out=sums[r],
                     lhsT=w2_codes[:, r * P : (r + 1) * P].bitcast(FP8X4),
                     lhsT_scale=w2_plane[:, r * P : (r + 1) * P],
-                    rhs=z_codes[:].bitcast(FP8X4),
+                    rhs=z_codes[c][:].bitcast(FP8X4),
                     rhs_scale=z_scales[:],
                     start=True,
                     stop=True,
@@ -303,3 +296,13 @@ def tile_picked_inorm_none_e_kernel(tc, xT, w1, w2_words, w2_scales, gamma, offs
             if c in stores:
                 a, b = stores[c]
                 nc.sync.dma_start(out=out_rows[:, :, a:b], in_=result[:, :, a:b])
+
+        join_z(True, 0, 0, QUARTER)
+        join_z(False, 2, 0, QUARTER)
+        join_z(True, 1, 0, QUARTER)
+        join_z(False, 3, 0, LAST_JOIN_ON_SCALAR)
+        second_product(0)
+        join_z(True, 3, LAST_JOIN_ON_SCALAR, QUARTER)
+        second_product(1)
+        second_product(2)
+        second_product(3)

@@ -21,14 +21,15 @@ K_PASS = P * PACK
 PASSES = K // K_PASS
 HALF = S // 2
 QUARTER = S // 4
+SUMMED = 1
 LAST = PACK - 1
 EPS = 1e-5
 ALIGN = 64
-LAST_JOIN_ON_SCALAR = 48
 NARROW = 32
 
 JOIN_ON_VECTOR = (256, 352)
 W_ON_SCALAR = ((44, 96), (44, 52))
+LAST_JOIN_ON_SCALAR = 48
 
 
 def tile_picked_inorm_none_e_kernel(tc, xT, w1, w2_words, w2_scales, gamma, offs, out):
@@ -46,8 +47,8 @@ def tile_picked_inorm_none_e_kernel(tc, xT, w1, w2_words, w2_scales, gamma, offs
         else:
             nc.scalar.copy(out=dst, in_=src)
 
-    def interleave(copy, on_vector, dst, src, i=4):
-        copy(on_vector, dst.rearrange("p (c i) r -> p c r i", i=i), src.rearrange("p r (c i) -> p c r i", i=i))
+    def interleave(copy, on_vector, dst, src):
+        copy(on_vector, dst.rearrange("p (c i) r -> p c r i", i=4), src.rearrange("p r (c i) -> p c r i", i=4))
 
     with ExitStack() as ctx:
         keep = ctx.enter_context(tc.tile_pool(name="keep", bufs=1))
@@ -61,8 +62,8 @@ def tile_picked_inorm_none_e_kernel(tc, xT, w1, w2_words, w2_scales, gamma, offs
         nc.gpsimd.memset(w2_plane[:].bitcast(U32), 0)
         nc.vector.memset(preload[:, 0:1], 1.0)
         nc.scalar.activation(out=preload[:, 1:2], in_=preload[:, 0:1], func=ACT.Abs_reciprocal_sqrt)
-        nc.vector.memset(moments[:, :, 0:1], -1.0)
-        nc.vector.memset(moments[:, 1, 0:1], -float(S))
+        for t in range(PACK):
+            nc.vector.memset(moments[:, t, 0:1], -float(S) if t == SUMMED else -1.0)
 
         def load_scale_rows(q):
             nc.sync.dma_start(out=w2_plane[32 * q : 32 * q + 4, :].bitcast(I32), in_=w2_scales[0, 4 * q : 4 * q + 4, :].bitcast(I32))
@@ -89,35 +90,34 @@ def tile_picked_inorm_none_e_kernel(tc, xT, w1, w2_words, w2_scales, gamma, offs
         joined = [keep.tile([P, S, PACK], BF16, name=f"x_joined_{g}", align_bytes=ALIGN) for g in range(PASSES)]
         first_codes = keep.tile([P, S], U32, name="x_codes_0", align_bytes=ALIGN)
         first_scales = keep.tile([P, S], U8, name="x_scales_0", align_bytes=ALIGN)
-        late_codes = {}
-        late_scales = {}
+        second_codes = {}
+        second_scales = {}
 
-        def quantise_points(g, n, tag):
-            cols = slice(n * HALF, (n + 1) * HALF)
-            if g == 0:
-                codes, plane = first_codes[:, cols], first_scales[:, cols]
-            else:
-                late_codes[n] = keep.tile([P, HALF], U32, name=f"x_codes_1_{n}", tag=tag, align_bytes=ALIGN)
-                late_scales[n] = keep.tile([P, HALF], U8, name=f"x_scales_1_{n}", align_bytes=ALIGN)
-                codes, plane = late_codes[n][:], late_scales[n][:]
-            nc.vector.quantize_mx(out=codes.bitcast(FP8X4), scales=plane, in_=joined[g][:, cols, :].rearrange("p n j -> p (n j)"))
+        def quantise_points(g, n, codes, scales):
+            values = joined[g][:, n * HALF : (n + 1) * HALF, :].rearrange("p n j -> p (n j)")
+            nc.vector.quantize_mx(out=codes.bitcast(FP8X4), scales=scales, in_=values)
 
-        found = {}
+        def quantise_second_pass(n, tag):
+            second_codes[n] = keep.tile([P, HALF], U32, name=f"x_codes_1_{n}", tag=tag, align_bytes=ALIGN)
+            second_scales[n] = keep.tile([P, HALF], U8, name=f"x_scales_1_{n}", align_bytes=ALIGN)
+            quantise_points(1, n, second_codes[n][:], second_scales[n][:])
+
         for g in range(PASSES):
-            found[g] = keep.tile([P, PACK, S], F32, name=f"x_found_{g}", align_bytes=ALIGN)
+            found = keep.tile([P, PACK, S], F32, name=f"x_found_{g}", align_bytes=ALIGN)
             for u in range(2):
                 for a, b in [(0, HALF), (HALF, S)] if (g, u) == (1, 1) else [(0, S)]:
                     part = offsets[:, a // 16 : b // 16]
-                    nc.vector.tensor_copy(out=found[g][:, 2 * u, a:b], in_=x_raw[g, u][:, 0, :].indirect(part))
-                    nc.scalar.activation(out=found[g][:, 2 * u + 1, a:b], in_=x_raw[g, u][:, 1, :].indirect(part), func=ACT.Copy)
+                    for r in range(2):
+                        copy_floats(r == 0, found[:, 2 * u + r, a:b], x_raw[g, u][:, r, :].indirect(part))
             cut = JOIN_ON_VECTOR[g]
-            interleave(copy_floats, True, joined[g][:, 0:HALF, :], found[g][:, :, 0:HALF])
+            interleave(copy_floats, True, joined[g][:, 0:HALF, :], found[:, :, 0:HALF])
             if cut > HALF:
-                interleave(copy_floats, True, joined[g][:, HALF:cut, :], found[g][:, :, HALF:cut])
-            interleave(copy_floats, False, joined[g][:, cut:S, :], found[g][:, :, cut:S])
+                interleave(copy_floats, True, joined[g][:, HALF:cut, :], found[:, :, HALF:cut])
+            interleave(copy_floats, False, joined[g][:, cut:S, :], found[:, :, cut:S])
             if g == 0:
                 for n in range(2):
-                    quantise_points(0, n, None)
+                    cols = slice(n * HALF, (n + 1) * HALF)
+                    quantise_points(0, n, first_codes[:, cols], first_scales[:, cols])
 
         dealt = {}
         w_codes = {}
@@ -128,45 +128,35 @@ def tile_picked_inorm_none_e_kernel(tc, xT, w1, w2_words, w2_scales, gamma, offs
             dealt[g, u] = keep.tile([P, 2, P, PACK], BF16, name=f"w_dealt_{g}_{u}", align_bytes=ALIGN)
             dst = dealt[g, u][:].rearrange("p s m j -> p m j s")
             src = w_raw[g][:].rearrange("p j (m t) -> p m j t", t=PACK)[:, :, :, 2 * u : 2 * u + 2]
-            if cut > 0:
-                copy_floats(False, dst[:, 0:cut], src[:, 0:cut])
-            if cut < P:
-                copy_floats(True, dst[:, cut:P], src[:, cut:P])
+            copy_floats(False, dst[:, 0:cut], src[:, 0:cut])
+            copy_floats(True, dst[:, cut:P], src[:, cut:P])
 
-        def quantise_weights(g, u, spans):
-            for s0, s1 in spans:
-                codes = keep.tile([P, (s1 - s0) * P], U32, name=f"w_codes_{g}_{u}_{s0}", align_bytes=ALIGN)
-                plane = keep.tile([P, (s1 - s0) * P], U8, name=f"w_scales_{g}_{u}_{s0}", align_bytes=ALIGN)
-                nc.vector.quantize_mx(
-                    out=codes[:].bitcast(FP8X4),
-                    scales=plane[:],
-                    in_=dealt[g, u][:, s0:s1].rearrange("p s m j -> p (s m j)"),
-                )
-                for s in range(s0, s1):
-                    w_codes[g, 2 * u + s] = codes[:, (s - s0) * P : (s - s0 + 1) * P]
-                    w_scales[g, 2 * u + s] = plane[:, (s - s0) * P : (s - s0 + 1) * P]
+        def quantise_weights(g, u, s0, s1):
+            codes = keep.tile([P, (s1 - s0) * P], U32, name=f"w_codes_{g}_{u}_{s0}", align_bytes=ALIGN)
+            scales = keep.tile([P, (s1 - s0) * P], U8, name=f"w_scales_{g}_{u}_{s0}", align_bytes=ALIGN)
+            nc.vector.quantize_mx(out=codes[:].bitcast(FP8X4), scales=scales[:], in_=dealt[g, u][:, s0:s1].rearrange("p s m j -> p (s m j)"))
+            for s in range(s0, s1):
+                w_codes[g, 2 * u + s] = codes[:, (s - s0) * P : (s - s0 + 1) * P]
+                w_scales[g, 2 * u + s] = scales[:, (s - s0) * P : (s - s0 + 1) * P]
 
-        quantise_points(1, 0, "x_codes_1_0")
+        quantise_second_pass(0, "x_codes_1_0")
         deal_weights(0, 0)
-        quantise_weights(0, 0, [(0, 2)])
+        quantise_weights(0, 0, 0, 2)
         deal_weights(0, 1)
-        quantise_points(1, 1, "w_dealt_0_0")
-        quantise_weights(0, 1, [(0, 2)])
+        quantise_second_pass(1, "w_dealt_0_0")
+        quantise_weights(0, 1, 0, 2)
         for u in range(2):
             deal_weights(1, u)
-        quantise_weights(1, 0, [(0, 1), (1, 2)])
-        quantise_weights(1, 1, [(0, 1), (1, 2)])
+        for t in range(PACK):
+            quantise_weights(1, t // 2, t % 2, t % 2 + 1)
 
-        spans = {t: [(0, S)] for t in range(LAST)}
-        spans[0] = spans[2] = spans[LAST] = [(0, HALF), (HALF, S)]
-
-        def warm_up(tag, codes, plane):
+        def warm_up(tag, codes, scales):
             idle = psum.tile([NARROW, S], F32, name="idle_" + tag, tag=tag)
             for r in range(2):
                 nc.tensor.matmul_mx(
                     out=idle[:],
                     lhsT=codes[:, r * P : r * P + NARROW].bitcast(FP8X4),
-                    lhsT_scale=plane[:, r * P : r * P + NARROW],
+                    lhsT_scale=scales[:, r * P : r * P + NARROW],
                     rhs=first_codes[:].bitcast(FP8X4),
                     rhs_scale=first_scales[:],
                     start=True,
@@ -176,6 +166,8 @@ def tile_picked_inorm_none_e_kernel(tc, xT, w1, w2_words, w2_scales, gamma, offs
         warm_up("acc_0", first_codes, w2_plane)
         for q in range(1, 4):
             load_scale_rows(q)
+
+        spans = {t: [(0, S)] if t == SUMMED else [(0, HALF), (HALF, S)] for t in range(PACK)}
         banks = {(t, a): psum.tile([P, b - a], F32, name=f"h_{t}_{a}") for t in range(PACK) for a, b in spans[t]}
         for t in range(PACK):
             for a, b in spans[t]:
@@ -190,18 +182,17 @@ def tile_picked_inorm_none_e_kernel(tc, xT, w1, w2_words, w2_scales, gamma, offs
                 )
         for t in range(PACK):
             for n in range(2):
-                split = len(spans[t]) == 2
                 nc.tensor.matmul_mx(
-                    out=banks[t, n * HALF][:] if split else banks[t, 0][:, n * HALF : (n + 1) * HALF],
+                    out=banks[t, 0][:, n * HALF : (n + 1) * HALF] if t == SUMMED else banks[t, n * HALF][:],
                     lhsT=w_codes[1, t].bitcast(FP8X4),
                     lhsT_scale=w_scales[1, t],
-                    rhs=late_codes[n][:].bitcast(FP8X4),
-                    rhs_scale=late_scales[n][:],
+                    rhs=second_codes[n][:].bitcast(FP8X4),
+                    rhs_scale=second_scales[n][:],
                     start=False,
-                    stop=split or n == 1,
+                    stop=t != SUMMED or n == 1,
                 )
 
-        stats = [keep.tile([P, len(spans[t]), 6], F32, name=f"stats_{t}") for t in range(PACK)]
+        stats = {t: keep.tile([P, 2, 6], F32, name=f"stats_{t}") for t in range(PACK) if t != SUMMED}
         rstd = keep.tile([P, PACK], F32, name="rstd")
         factors = [keep.tile([P, 2], F32, name=f"factors_{t}") for t in range(PACK)]
         minus_gam = keep.tile([P, PACK], F32, name="minus_gam")
@@ -210,55 +201,64 @@ def tile_picked_inorm_none_e_kernel(tc, xT, w1, w2_words, w2_scales, gamma, offs
         z_joined = [keep.tile([P, QUARTER, PACK], BF16, name=f"z_joined_{c}", align_bytes=ALIGN) for c in range(4)]
         nc.scalar.activation(out=minus_gam[:], in_=gam[:], func=ACT.Copy, scale=-1.0)
 
-        def make_factors(engine, t, signed_gam):
-            engine.tensor_scalar(
-                out=factors[t][:], in0=moments[:, t, 0:2], scalar1=rstd[:, t : t + 1], scalar2=signed_gam[:, t : t + 1], op0=ALU.mult, op1=ALU.mult
-            )
+        def statistics(t, n):
+            nc.vector.bn_stats(out=stats[t][:, n, :], in_=banks[t, n * HALF][:])
 
-        def close(t):
+        def close_statistics(t):
             nc.vector.bn_aggr(out=moments[:, t, 1:3], in_=stats[t][:].rearrange("p n s -> p (n s)"))
             nc.scalar.activation(out=rstd[:, t : t + 1], in_=moments[:, t, 2:3], func=ACT.Abs_reciprocal_sqrt, bias=EPS)
 
-        def normalise(on_vector, t, a, b, src):
+        def make_factors(t):
+            signed_gam = gam if t == SUMMED else minus_gam
+            nc.vector.tensor_scalar(
+                out=factors[t][:],
+                in0=moments[:, t, 0:2],
+                scalar1=rstd[:, t : t + 1],
+                scalar2=signed_gam[:, t : t + 1],
+                op0=ALU.mult,
+                op1=ALU.mult,
+            )
+
+        def normalise(on_vector, t, a, b, values):
+            scale, bias = factors[t][:, 0:1], factors[t][:, 1:2]
             if on_vector:
-                nc.vector.tensor_scalar(
-                    out=z_planes[:, t, a:b], in0=src, scalar1=factors[t][:, 0:1], scalar2=factors[t][:, 1:2], op0=ALU.mult, op1=ALU.add
-                )
+                nc.vector.tensor_scalar(out=z_planes[:, t, a:b], in0=values, scalar1=scale, scalar2=bias, op0=ALU.mult, op1=ALU.add)
             else:
-                nc.scalar.activation(out=z_planes[:, t, a:b], in_=src, func=ACT.Identity, scale=factors[t][:, 0:1], bias=factors[t][:, 1:2])
+                nc.scalar.activation(out=z_planes[:, t, a:b], in_=values, func=ACT.Identity, scale=scale, bias=bias)
 
-        def part_statistics(t, n):
-            if len(spans[t]) == 1:
-                nc.vector.bn_stats(out=stats[t][:, n, :], in_=banks[t, 0][:, n * HALF : (n + 1) * HALF])
-            else:
-                nc.vector.bn_stats(out=stats[t][:, n, :], in_=banks[t, n * HALF][:])
-
-        part_statistics(0, 0)
-        part_statistics(0, 1)
-        nc.scalar.activation(out=h_copy[:], in_=banks[1, 0][:], func=ACT.Copy, scale=-1.0 / S, accum_out=moments[:, 1, 1:2])
-        part_statistics(2, 0)
-        close(0)
-        part_statistics(2, 1)
-        nc.scalar.activation(out=z_planes[:, 1, :], in_=banks[1, 0][:], func=ACT.Square, bias=moments[:, 1, 1:2], accum_out=moments[:, 1, 2:3])
-        part_statistics(LAST, 0)
-        make_factors(nc.vector, 0, minus_gam)
-        close(2)
-        part_statistics(LAST, 1)
-        nc.scalar.activation(out=rstd[:, 1:2], in_=moments[:, 1, 2:3], func=ACT.Abs_reciprocal_sqrt, scale=1.0 / S, bias=EPS)
-        make_factors(nc.vector, 2, minus_gam)
+        statistics(0, 0)
+        statistics(0, 1)
+        nc.scalar.activation(out=h_copy[:], in_=banks[SUMMED, 0][:], func=ACT.Copy, scale=-1.0 / S, accum_out=moments[:, SUMMED, 1:2])
+        statistics(2, 0)
+        close_statistics(0)
+        statistics(2, 1)
+        nc.scalar.activation(
+            out=z_planes[:, SUMMED, :],
+            in_=banks[SUMMED, 0][:],
+            func=ACT.Square,
+            bias=moments[:, SUMMED, 1:2],
+            accum_out=moments[:, SUMMED, 2:3],
+        )
+        statistics(LAST, 0)
+        make_factors(0)
+        close_statistics(2)
+        statistics(LAST, 1)
+        nc.scalar.activation(
+            out=rstd[:, SUMMED : SUMMED + 1], in_=moments[:, SUMMED, 2:3], func=ACT.Abs_reciprocal_sqrt, scale=1.0 / S, bias=EPS
+        )
+        make_factors(2)
         normalise(False, 0, 0, HALF, banks[0, 0][:])
-        warm_up("h_0_0", late_codes[0], late_scales[0])
-        close(LAST)
-        make_factors(nc.vector, 1, gam)
+        warm_up("h_0_0", second_codes[0], second_scales[0])
+        close_statistics(LAST)
+        make_factors(SUMMED)
         normalise(False, 0, HALF, S, banks[0, HALF][:])
         normalise(True, 2, 0, HALF, banks[2, 0][:])
-        make_factors(nc.vector, LAST, minus_gam)
-        normalise(True, 1, 0, S, h_copy[:])
+        make_factors(LAST)
+        normalise(True, SUMMED, 0, S, h_copy[:])
         normalise(False, 2, HALF, S, banks[2, HALF][:])
         normalise(True, LAST, 0, QUARTER, banks[LAST, 0][:, 0:QUARTER])
         normalise(True, LAST, QUARTER, HALF, banks[LAST, 0][:, QUARTER:HALF])
         normalise(False, LAST, HALF, S, banks[LAST, HALF][:])
-
 
         def join_z(on_vector, c, a, b):
             interleave(copy_bits, on_vector, z_joined[c][:, a:b, :], z_planes[:, :, c * QUARTER + a : c * QUARTER + b])
@@ -267,12 +267,12 @@ def tile_picked_inorm_none_e_kernel(tc, xT, w1, w2_words, w2_scales, gamma, offs
         out_rows = out.rearrange("(r p) n -> p r n", p=P)
         result = keep.tile([P, 2, S], F32, name="result")
         stores = {0: (0, QUARTER), 2: (QUARTER, 3 * QUARTER), 3: (3 * QUARTER, S)}
-        z_codes = [keep.tile([P, QUARTER], U32, name=f"z_codes_{c}", align_bytes=ALIGN) for c in range(4)]
 
         def second_product(c):
             cols = slice(c * QUARTER, (c + 1) * QUARTER)
+            z_codes = keep.tile([P, QUARTER], U32, name=f"z_codes_{c}", align_bytes=ALIGN)
             z_scales = keep.tile([P, QUARTER], U8, name=f"z_scales_{c}", align_bytes=ALIGN)
-            nc.vector.quantize_mx(out=z_codes[c][:].bitcast(FP8X4), scales=z_scales[:], in_=z_joined[c][:].rearrange("p n t -> p (n t)"))
+            nc.vector.quantize_mx(out=z_codes[:].bitcast(FP8X4), scales=z_scales[:], in_=z_joined[c][:].rearrange("p n t -> p (n t)"))
             if c == 0:
                 shared = psum.tile([P, 2, QUARTER], F32, name="acc_0")
                 sums = [shared[:, r, :] for r in range(2)]
@@ -283,7 +283,7 @@ def tile_picked_inorm_none_e_kernel(tc, xT, w1, w2_words, w2_scales, gamma, offs
                     out=sums[r],
                     lhsT=w2_codes[:, r * P : (r + 1) * P].bitcast(FP8X4),
                     lhsT_scale=w2_plane[:, r * P : (r + 1) * P],
-                    rhs=z_codes[c][:].bitcast(FP8X4),
+                    rhs=z_codes[:].bitcast(FP8X4),
                     rhs_scale=z_scales[:],
                     start=True,
                     stop=True,
@@ -303,6 +303,5 @@ def tile_picked_inorm_none_e_kernel(tc, xT, w1, w2_words, w2_scales, gamma, offs
         join_z(False, 3, 0, LAST_JOIN_ON_SCALAR)
         second_product(0)
         join_z(True, 3, LAST_JOIN_ON_SCALAR, QUARTER)
-        second_product(1)
-        second_product(2)
-        second_product(3)
+        for c in range(1, 4):
+            second_product(c)

@@ -29,7 +29,7 @@ NARROW = 32
 
 JOIN_ON_VECTOR = (256, 352)
 W_ON_SCALAR = ((44, 96), (44, 52))
-LAST_JOIN_ON_SCALAR = 48
+LAST_JOIN_ON_SCALAR = 32
 
 
 def tile_picked_inorm_none_e_kernel(tc, xT, w1, w2_words, w2_scales, gamma, offs, out):
@@ -197,7 +197,11 @@ def tile_picked_inorm_none_e_kernel(tc, xT, w1, w2_words, w2_scales, gamma, offs
         factors = [keep.tile([P, 2], F32, name=f"factors_{t}") for t in range(PACK)]
         minus_gam = keep.tile([P, PACK], F32, name="minus_gam")
         h_copy = keep.tile([P, S], F32, name="h_copy")
-        z_planes = keep.tile([P, PACK, S], BF16, name="z_planes", align_bytes=ALIGN)
+        z_halves = [keep.tile([P, PACK, HALF], BF16, name=f"z_planes_{n}", align_bytes=ALIGN) for n in range(2)]
+
+        def z_plane(t, a, b):
+            return z_halves[a // HALF][:, t, a % HALF : a % HALF + b - a]
+
         z_joined = [keep.tile([P, QUARTER, PACK], BF16, name=f"z_joined_{c}", align_bytes=ALIGN) for c in range(4)]
         nc.scalar.activation(out=minus_gam[:], in_=gam[:], func=ACT.Copy, scale=-1.0)
 
@@ -222,9 +226,27 @@ def tile_picked_inorm_none_e_kernel(tc, xT, w1, w2_words, w2_scales, gamma, offs
         def normalise(on_vector, t, a, b, values):
             scale, bias = factors[t][:, 0:1], factors[t][:, 1:2]
             if on_vector:
-                nc.vector.tensor_scalar(out=z_planes[:, t, a:b], in0=values, scalar1=scale, scalar2=bias, op0=ALU.mult, op1=ALU.add)
+                nc.vector.tensor_scalar(out=z_plane(t, a, b), in0=values, scalar1=scale, scalar2=bias, op0=ALU.mult, op1=ALU.add)
             else:
-                nc.scalar.activation(out=z_planes[:, t, a:b], in_=values, func=ACT.Identity, scale=scale, bias=bias)
+                nc.scalar.activation(out=z_plane(t, a, b), in_=values, func=ACT.Identity, scale=scale, bias=bias)
+
+        h_scaled = keep.tile([P, S], F32, name="h_scaled")
+        scaled_mean = keep.tile([P, 1], F32, name="scaled_mean")
+
+        def copy_scaled(n):
+            nc.scalar.activation(
+                out=h_scaled[:, n * HALF : (n + 1) * HALF], in_=banks[LAST, n * HALF][:], func=ACT.Copy, scale=gam[:, LAST : LAST + 1]
+            )
+
+        def normalise_last(a, b):
+            nc.vector.tensor_scalar(
+                out=z_plane(LAST, a, b),
+                in0=h_scaled[:, a:b],
+                scalar1=scaled_mean[:],
+                scalar2=rstd[:, LAST : LAST + 1],
+                op0=ALU.subtract,
+                op1=ALU.mult,
+            )
 
         statistics(0, 0)
         statistics(0, 1)
@@ -233,7 +255,7 @@ def tile_picked_inorm_none_e_kernel(tc, xT, w1, w2_words, w2_scales, gamma, offs
         close_statistics(0)
         statistics(2, 1)
         nc.scalar.activation(
-            out=z_planes[:, SUMMED, :],
+            out=h_scaled[:],
             in_=banks[SUMMED, 0][:],
             func=ACT.Square,
             bias=moments[:, SUMMED, 1:2],
@@ -249,24 +271,26 @@ def tile_picked_inorm_none_e_kernel(tc, xT, w1, w2_words, w2_scales, gamma, offs
         make_factors(2)
         normalise(False, 0, 0, HALF, banks[0, 0][:])
         warm_up("h_0_0", second_codes[0], second_scales[0])
+        copy_scaled(0)
         close_statistics(LAST)
+        nc.scalar.activation(out=scaled_mean[:], in_=moments[:, LAST, 1:2], func=ACT.Copy, scale=gam[:, LAST : LAST + 1])
         make_factors(SUMMED)
-        normalise(False, 0, HALF, S, banks[0, HALF][:])
         normalise(True, 2, 0, HALF, banks[2, 0][:])
+        normalise(True, SUMMED, 0, HALF, h_copy[:, 0:HALF])
+        normalise(False, 0, HALF, S, banks[0, HALF][:])
         make_factors(LAST)
-        normalise(True, SUMMED, 0, S, h_copy[:])
+        normalise_last(0, HALF)
         normalise(False, 2, HALF, S, banks[2, HALF][:])
-        normalise(True, LAST, 0, QUARTER, banks[LAST, 0][:, 0:QUARTER])
-        normalise(True, LAST, QUARTER, HALF, banks[LAST, 0][:, QUARTER:HALF])
+        normalise(True, SUMMED, HALF, S, h_copy[:, HALF:S])
         normalise(False, LAST, HALF, S, banks[LAST, HALF][:])
 
         def join_z(on_vector, c, a, b):
-            interleave(copy_bits, on_vector, z_joined[c][:, a:b, :], z_planes[:, :, c * QUARTER + a : c * QUARTER + b])
+            interleave(copy_bits, on_vector, z_joined[c][:, a:b, :], z_halves[c // 2][:, :, c % 2 * QUARTER + a : c % 2 * QUARTER + b])
 
         banks_of = {1: ("h_1_0", "h_0_0"), 2: ("h_2_0", "h_0_256"), 3: ("h_2_256", "h_3_0")}
         out_rows = out.rearrange("(r p) n -> p r n", p=P)
         result = keep.tile([P, 2, S], F32, name="result")
-        stores = {0: (0, QUARTER), 2: (QUARTER, 3 * QUARTER), 3: (3 * QUARTER, S)}
+        stores = {0: (0, QUARTER), 1: (QUARTER, HALF), 3: (HALF, S)}
 
         def second_product(c):
             cols = slice(c * QUARTER, (c + 1) * QUARTER)

@@ -287,7 +287,7 @@ def tile_picked_inorm_none_e_kernel(tc, xT, w1, w2_words, w2_scales, gamma, offs
         def join_z(on_vector, c, a, b):
             interleave(copy_bits, on_vector, z_joined[c][:, a:b, :], z_halves[c // 2][:, :, c % 2 * QUARTER + a : c % 2 * QUARTER + b])
 
-        banks_of = {1: ("h_1_0", "h_0_0"), 2: ("h_2_0", "h_0_256"), 3: ("h_2_256", "h_3_0")}
+        banks_of = {0: ("acc_0", "h_1_0"), 1: ("h_3_0", "h_0_0"), 2: ("h_2_0", "h_0_256"), 3: ("h_2_256", "h_3_256")}
         out_rows = out.rearrange("(r p) n -> p r n", p=P)
         result = keep.tile([P, 2, S], F32, name="result")
         stores = {0: (0, QUARTER), 1: (QUARTER, HALF), 3: (HALF, S)}
@@ -297,11 +297,7 @@ def tile_picked_inorm_none_e_kernel(tc, xT, w1, w2_words, w2_scales, gamma, offs
             z_codes = keep.tile([P, QUARTER], U32, name=f"z_codes_{c}", align_bytes=ALIGN)
             z_scales = keep.tile([P, QUARTER], U8, name=f"z_scales_{c}", align_bytes=ALIGN)
             nc.vector.quantize_mx(out=z_codes[:].bitcast(FP8X4), scales=z_scales[:], in_=z_joined[c][:].rearrange("p n t -> p (n t)"))
-            if c == 0:
-                shared = psum.tile([P, 2, QUARTER], F32, name="acc_0")
-                sums = [shared[:, r, :] for r in range(2)]
-            else:
-                sums = [psum.tile([P, QUARTER], F32, name=f"acc_{c}_{r}", tag=banks_of[c][r])[:] for r in range(2)]
+            sums = [psum.tile([P, QUARTER], F32, name=f"acc_{c}_{r}", tag=banks_of[c][r])[:] for r in range(2)]
             for r in range(2):
                 nc.tensor.matmul_mx(
                     out=sums[r],
@@ -312,11 +308,8 @@ def tile_picked_inorm_none_e_kernel(tc, xT, w1, w2_words, w2_scales, gamma, offs
                     start=True,
                     stop=True,
                 )
-            if c == 0:
-                copy_floats(False, result[:, :, cols], shared[:])
-            else:
-                for r in range(2):
-                    copy_floats(r == 1, result[:, r, cols], sums[r])
+            for r in range(2):
+                copy_floats(r == 1 and c > 0, result[:, r, cols], sums[r])
             if c in stores:
                 a, b = stores[c]
                 nc.sync.dma_start(out=out_rows[:, :, a:b], in_=result[:, :, a:b])

@@ -270,8 +270,8 @@ def tile_picked_inorm_none_e_kernel(tc, xT, w1, w2_words, w2_scales, gamma, offs
         )
         make_factors(2)
         normalise(False, 0, 0, HALF, banks[0, 0][:])
-        warm_up("h_0_0", second_codes[0], second_scales[0])
         copy_scaled(0)
+        warm_up("h_3_0", second_codes[0], second_scales[0])
         close_statistics(LAST)
         nc.scalar.activation(out=scaled_mean[:], in_=moments[:, LAST, 1:2], func=ACT.Copy, scale=gam[:, LAST : LAST + 1])
         make_factors(SUMMED)

@@ -27,7 +27,7 @@ EPS = 1e-5
 ALIGN = 64
 NARROW = 32
 
-JOIN_ON_VECTOR = (256, 352)
+JOIN_ON_VECTOR = (320, 352)
 W_ON_SCALAR = ((44, 96), (44, 52))
 LAST_JOIN_ON_SCALAR = 32
 
@@ -273,16 +273,18 @@ def tile_picked_inorm_none_e_kernel(tc, xT, w1, w2_words, w2_scales, gamma, offs
         copy_scaled(0)
         warm_up("h_3_0", second_codes[0], second_scales[0])
         close_statistics(LAST)
-        nc.scalar.activation(out=scaled_mean[:], in_=moments[:, LAST, 1:2], func=ACT.Copy, scale=gam[:, LAST : LAST + 1])
         make_factors(SUMMED)
         normalise(True, 2, 0, HALF, banks[2, 0][:])
+        nc.vector.tensor_scalar(out=scaled_mean[:], in0=moments[:, LAST, 1:2], scalar1=gam[:, LAST : LAST + 1], scalar2=None, op0=ALU.mult)
         normalise(True, SUMMED, 0, HALF, h_copy[:, 0:HALF])
         normalise(False, 0, HALF, S, banks[0, HALF][:])
         make_factors(LAST)
-        normalise_last(0, HALF)
+        normalise_last(0, QUARTER)
+        normalise_last(QUARTER, HALF)
         normalise(False, 2, HALF, S, banks[2, HALF][:])
         normalise(True, SUMMED, HALF, S, h_copy[:, HALF:S])
-        normalise(False, LAST, HALF, S, banks[LAST, HALF][:])
+        normalise(False, LAST, HALF, 3 * QUARTER, banks[LAST, HALF][:, 0:QUARTER])
+        normalise(False, LAST, 3 * QUARTER, S, banks[LAST, HALF][:, QUARTER:HALF])
 
         def join_z(on_vector, c, a, b):
             interleave(copy_bits, on_vector, z_joined[c][:, a:b, :], z_halves[c // 2][:, :, c % 2 * QUARTER + a : c % 2 * QUARTER + b])

@@ -133,8 +133,11 @@ def tile_picked_inorm_none_e_kernel(tc, xT, w1, w2_words, w2_scales, gamma, offs
 
         def quantise_weights(g, u, s0, s1):
             codes = keep.tile([P, (s1 - s0) * P], U32, name=f"w_codes_{g}_{u}_{s0}", align_bytes=ALIGN)
-            scales = keep.tile([P, (s1 - s0) * P], U8, name=f"w_scales_{g}_{u}_{s0}", align_bytes=ALIGN)
-            nc.vector.quantize_mx(out=codes[:].bitcast(FP8X4), scales=scales[:], in_=dealt[g, u][:, s0:s1].rearrange("p s m j -> p (s m j)"))
+            if (g, 2 * u + s0) == (1, 2):
+                scales = w_scales[0, LAST][PACK:P, :]
+            else:
+                scales = keep.tile([P, (s1 - s0) * P], U8, name=f"w_scales_{g}_{u}_{s0}", align_bytes=ALIGN)[:]
+            nc.vector.quantize_mx(out=codes[:].bitcast(FP8X4), scales=scales, in_=dealt[g, u][:, s0:s1].rearrange("p s m j -> p (s m j)"))
             for s in range(s0, s1):
                 w_codes[g, 2 * u + s] = codes[:, (s - s0) * P : (s - s0 + 1) * P]
                 w_scales[g, 2 * u + s] = scales[:, (s - s0) * P : (s - s0 + 1) * P]
@@ -169,19 +172,25 @@ def tile_picked_inorm_none_e_kernel(tc, xT, w1, w2_words, w2_scales, gamma, offs
 
         spans = {t: [(0, S)] if t == SUMMED else [(0, HALF), (HALF, S)] for t in range(PACK)}
         banks = {(t, a): psum.tile([P, b - a], F32, name=f"h_{t}_{a}") for t in range(PACK) for a, b in spans[t]}
-        for t in range(PACK):
+
+        def first_pass(t, a, b):
+            nc.tensor.matmul_mx(
+                out=banks[t, a][:],
+                lhsT=w_codes[0, t].bitcast(FP8X4),
+                lhsT_scale=w_scales[0, t],
+                rhs=first_codes[:, a:b].bitcast(FP8X4),
+                rhs_scale=first_scales[:, a:b],
+                start=True,
+                stop=False,
+            )
+
+        for t in range(LAST):
             for a, b in spans[t]:
-                nc.tensor.matmul_mx(
-                    out=banks[t, a][:],
-                    lhsT=w_codes[0, t].bitcast(FP8X4),
-                    lhsT_scale=w_scales[0, t],
-                    rhs=first_codes[:, a:b].bitcast(FP8X4),
-                    rhs_scale=first_scales[:, a:b],
-                    start=True,
-                    stop=False,
-                )
+                first_pass(t, a, b)
         for t in range(PACK):
             for n in range(2):
+                if t == LAST:
+                    first_pass(t, n * HALF, (n + 1) * HALF)
                 nc.tensor.matmul_mx(
                     out=banks[t, 0][:, n * HALF : (n + 1) * HALF] if t == SUMMED else banks[t, n * HALF][:],
                     lhsT=w_codes[1, t].bitcast(FP8X4),

@@ -29,7 +29,7 @@ NARROW = 32
 
 JOIN_ON_VECTOR = (320, 352)
 W_ON_SCALAR = ((44, 96), (44, 52))
-LAST_JOIN_ON_SCALAR = 32
+LAST_JOIN_ON_SCALAR = 56
 
 
 def tile_picked_inorm_none_e_kernel(tc, xT, w1, w2_words, w2_scales, gamma, offs, out):
@@ -133,11 +133,8 @@ def tile_picked_inorm_none_e_kernel(tc, xT, w1, w2_words, w2_scales, gamma, offs
 
         def quantise_weights(g, u, s0, s1):
             codes = keep.tile([P, (s1 - s0) * P], U32, name=f"w_codes_{g}_{u}_{s0}", align_bytes=ALIGN)
-            if (g, 2 * u + s0) == (1, 2):
-                scales = w_scales[0, LAST][PACK:P, :]
-            else:
-                scales = keep.tile([P, (s1 - s0) * P], U8, name=f"w_scales_{g}_{u}_{s0}", align_bytes=ALIGN)[:]
-            nc.vector.quantize_mx(out=codes[:].bitcast(FP8X4), scales=scales, in_=dealt[g, u][:, s0:s1].rearrange("p s m j -> p (s m j)"))
+            scales = keep.tile([P, (s1 - s0) * P], U8, name=f"w_scales_{g}_{u}_{s0}", align_bytes=ALIGN)
+            nc.vector.quantize_mx(out=codes[:].bitcast(FP8X4), scales=scales[:], in_=dealt[g, u][:, s0:s1].rearrange("p s m j -> p (s m j)"))
             for s in range(s0, s1):
                 w_codes[g, 2 * u + s] = codes[:, (s - s0) * P : (s - s0 + 1) * P]
                 w_scales[g, 2 * u + s] = scales[:, (s - s0) * P : (s - s0 + 1) * P]
@@ -172,25 +169,19 @@ def tile_picked_inorm_none_e_kernel(tc, xT, w1, w2_words, w2_scales, gamma, offs
 
         spans = {t: [(0, S)] if t == SUMMED else [(0, HALF), (HALF, S)] for t in range(PACK)}
         banks = {(t, a): psum.tile([P, b - a], F32, name=f"h_{t}_{a}") for t in range(PACK) for a, b in spans[t]}
-
-        def first_pass(t, a, b):
-            nc.tensor.matmul_mx(
-                out=banks[t, a][:],
-                lhsT=w_codes[0, t].bitcast(FP8X4),
-                lhsT_scale=w_scales[0, t],
-                rhs=first_codes[:, a:b].bitcast(FP8X4),
-                rhs_scale=first_scales[:, a:b],
-                start=True,
-                stop=False,
-            )
-
-        for t in range(LAST):
+        for t in range(PACK):
             for a, b in spans[t]:
-                first_pass(t, a, b)
+                nc.tensor.matmul_mx(
+                    out=banks[t, a][:],
+                    lhsT=w_codes[0, t].bitcast(FP8X4),
+                    lhsT_scale=w_scales[0, t],
+                    rhs=first_codes[:, a:b].bitcast(FP8X4),
+                    rhs_scale=first_scales[:, a:b],
+                    start=True,
+                    stop=False,
+                )
         for t in range(PACK):
             for n in range(2):
-                if t == LAST:
-                    first_pass(t, n * HALF, (n + 1) * HALF)
                 nc.tensor.matmul_mx(
                     out=banks[t, 0][:, n * HALF : (n + 1) * HALF] if t == SUMMED else banks[t, n * HALF][:],
                     lhsT=w_codes[1, t].bitcast(FP8X4),
@@ -244,7 +235,7 @@ def tile_picked_inorm_none_e_kernel(tc, xT, w1, w2_words, w2_scales, gamma, offs
 
         def copy_scaled(n):
             nc.scalar.activation(
-                out=h_scaled[:, n * HALF : (n + 1) * HALF], in_=banks[LAST, n * HALF][:], func=ACT.Copy, scale=gam[:, LAST : LAST + 1]
+                out=h_scaled[:, 0:QUARTER], in_=banks[LAST, 0][:, 0:QUARTER], func=ACT.Copy, scale=gam[:, LAST : LAST + 1]
             )
 
         def normalise_last(a, b):
@@ -278,9 +269,9 @@ def tile_picked_inorm_none_e_kernel(tc, xT, w1, w2_words, w2_scales, gamma, offs
             out=rstd[:, SUMMED : SUMMED + 1], in_=moments[:, SUMMED, 2:3], func=ACT.Abs_reciprocal_sqrt, scale=1.0 / S, bias=EPS
         )
         make_factors(2)
-        normalise(False, 0, 0, HALF, banks[0, 0][:])
         copy_scaled(0)
-        warm_up("h_3_0", second_codes[0], second_scales[0])
+        normalise(False, 0, 0, HALF, banks[0, 0][:])
+        warm_up("h_0_0", second_codes[0], second_scales[0])
         close_statistics(LAST)
         make_factors(SUMMED)
         normalise(True, 2, 0, HALF, banks[2, 0][:])
@@ -289,7 +280,7 @@ def tile_picked_inorm_none_e_kernel(tc, xT, w1, w2_words, w2_scales, gamma, offs
         normalise(False, 0, HALF, S, banks[0, HALF][:])
         make_factors(LAST)
         normalise_last(0, QUARTER)
-        normalise_last(QUARTER, HALF)
+        normalise(True, LAST, QUARTER, HALF, banks[LAST, 0][:, QUARTER:HALF])
         normalise(False, 2, HALF, S, banks[2, HALF][:])
         normalise(True, SUMMED, HALF, S, h_copy[:, HALF:S])
         normalise(False, LAST, HALF, 3 * QUARTER, banks[LAST, HALF][:, 0:QUARTER])

@@ -25,6 +25,7 @@ SUMMED = 1
 LAST = PACK - 1
 EPS = 1e-5
 ALIGN = 64
+DMA_ALIGN = 256
 NARROW = 32
 
 JOIN_ON_VECTOR = (320, 352)
@@ -72,19 +73,19 @@ def tile_picked_inorm_none_e_kernel(tc, xT, w1, w2_words, w2_scales, gamma, offs
         for g in range(PASSES):
             rows = xT[g * K_PASS : (g + 1) * K_PASS, :].rearrange("(p j) n -> p j n", j=PACK)
             for u in range(2):
-                x_raw[g, u] = keep.tile([P, 2, T], F32, name=f"x_raw_{g}_{u}", align_bytes=ALIGN)
+                x_raw[g, u] = keep.tile([P, 2, T], F32, name=f"x_raw_{g}_{u}", align_bytes=DMA_ALIGN)
                 nc.sync.dma_start(out=x_raw[g, u][:], in_=rows[:, 2 * u : 2 * u + 2, :])
                 if (g, u) == (0, 0):
                     nc.sync.dma_start(offsets[:], offs)
         w_raw = {}
         for g in range(PASSES):
-            w_raw[g] = keep.tile([P, PACK, H], F32, name=f"w_raw_{g}", align_bytes=ALIGN)
+            w_raw[g] = keep.tile([P, PACK, H], F32, name=f"w_raw_{g}", align_bytes=DMA_ALIGN)
             nc.sync.dma_start(out=w_raw[g][:], in_=w1[g * K_PASS : (g + 1) * K_PASS, :].rearrange("(p j) n -> p j n", j=PACK))
             if g == 0:
                 load_scale_rows(0)
         gam = keep.tile([P, PACK], F32, name="gam", align_bytes=ALIGN)
         nc.sync.dma_start(out=gam[:], in_=gamma.rearrange("(p t) o -> p (t o)", t=PACK))
-        w2_codes = keep.tile([P, N], U32, name="w2_codes", align_bytes=ALIGN)
+        w2_codes = keep.tile([P, N], U32, name="w2_codes", align_bytes=DMA_ALIGN)
         nc.sync.dma_start(out=w2_codes[:].bitcast(I32), in_=w2_words[0].rearrange("p n j -> p (n j)").bitcast(I32))
 
         joined = [keep.tile([P, S, PACK], BF16, name=f"x_joined_{g}", align_bytes=ALIGN) for g in range(PASSES)]
@@ -291,7 +292,7 @@ def tile_picked_inorm_none_e_kernel(tc, xT, w1, w2_words, w2_scales, gamma, offs
 
         banks_of = {0: ("acc_0", "h_1_0"), 1: ("h_3_0", "h_0_0"), 2: ("h_2_0", "h_0_256"), 3: ("h_2_256", "h_3_256")}
         out_rows = out.rearrange("(r p) n -> p r n", p=P)
-        result = keep.tile([P, 2, S], F32, name="result")
+        result = keep.tile([P, 2, S], F32, name="result", align_bytes=DMA_ALIGN)
         stores = {0: (0, QUARTER), 1: (QUARTER, HALF), 3: (HALF, S)}
 
         def second_product(c):

@@ -30,7 +30,7 @@ NARROW = 32
 
 JOIN_ON_VECTOR = (320, 352)
 W_ON_SCALAR = ((44, 96), (44, 52))
-LAST_JOIN_ON_SCALAR = 56
+LAST_JOIN_ON_SCALAR = 48
 
 
 def tile_picked_inorm_none_e_kernel(tc, xT, w1, w2_words, w2_scales, gamma, offs, out):

from contextlib import ExitStack

import concourse.mybir as mybir

K, T, S, H, N = 1024, 1024, 512, 512, 256
FLOPS = 2 * K * S * H + 2 * H * S * N

F32 = mybir.dt.float32
BF16 = mybir.dt.bfloat16
I32 = mybir.dt.int32
U32 = mybir.dt.uint32
U16 = mybir.dt.uint16
U8 = mybir.dt.uint8
FP8X4 = mybir.dt.float8_e4m3fn_x4
ACT = mybir.ActivationFunctionType
ALU = mybir.AluOpType

P = 128
PACK = 4
K_PASS = P * PACK
PASSES = K // K_PASS
HALF = S // 2
QUARTER = S // 4
SUMMED = 1
LAST = PACK - 1
EPS = 1e-5
ALIGN = 64
DMA_ALIGN = 256
NARROW = 32

JOIN_ON_VECTOR = (320, 352)
W_ON_SCALAR = ((44, 96), (44, 52))
LAST_JOIN_ON_SCALAR = 48


def tile_picked_inorm_none_e_kernel(tc, xT, w1, w2_words, w2_scales, gamma, offs, out):
    nc = tc.nc

    def copy_floats(on_vector, dst, src):
        if on_vector:
            nc.vector.tensor_copy(out=dst, in_=src)
        else:
            nc.scalar.activation(out=dst, in_=src, func=ACT.Copy)

    def copy_bits(on_vector, dst, src):
        if on_vector:
            nc.vector.tensor_copy(out=dst, in_=src)
        else:
            nc.scalar.copy(out=dst, in_=src)

    def interleave(copy, on_vector, dst, src):
        copy(on_vector, dst.rearrange("p (c i) r -> p c r i", i=4), src.rearrange("p r (c i) -> p c r i", i=4))

    with ExitStack() as ctx:
        keep = ctx.enter_context(tc.tile_pool(name="keep", bufs=1))
        psum = ctx.enter_context(tc.psum_pool(name="psum", bufs=1))

        offsets = keep.tile([P, S // 16], U16, name="offsets")
        w2_plane = keep.tile([P, N], U8, name="w2_plane", align_bytes=ALIGN)
        preload = keep.tile([P, 2], F32, name="preload")
        moments = keep.tile([P, PACK, 4], F32, name="moments")

        nc.gpsimd.memset(w2_plane[:].bitcast(U32), 0)
        nc.vector.memset(preload[:, 0:1], 1.0)
        nc.scalar.activation(out=preload[:, 1:2], in_=preload[:, 0:1], func=ACT.Abs_reciprocal_sqrt)
        for t in range(PACK):
            nc.vector.memset(moments[:, t, 0:1], -float(S) if t == SUMMED else -1.0)

        def load_scale_rows(q):
            nc.sync.dma_start(out=w2_plane[32 * q : 32 * q + 4, :].bitcast(I32), in_=w2_scales[0, 4 * q : 4 * q + 4, :].bitcast(I32))

        x_raw = {}
        for g in range(PASSES):
            rows = xT[g * K_PASS : (g + 1) * K_PASS, :].rearrange("(p j) n -> p j n", j=PACK)
            for u in range(2):
                x_raw[g, u] = keep.tile([P, 2, T], F32, name=f"x_raw_{g}_{u}", align_bytes=DMA_ALIGN)
                nc.sync.dma_start(out=x_raw[g, u][:], in_=rows[:, 2 * u : 2 * u + 2, :])
                if (g, u) == (0, 0):
                    nc.sync.dma_start(offsets[:], offs)
        w_raw = {}
        for g in range(PASSES):
            w_raw[g] = keep.tile([P, PACK, H], F32, name=f"w_raw_{g}", align_bytes=DMA_ALIGN)
            nc.sync.dma_start(out=w_raw[g][:], in_=w1[g * K_PASS : (g + 1) * K_PASS, :].rearrange("(p j) n -> p j n", j=PACK))
            if g == 0:
                load_scale_rows(0)
        gam = keep.tile([P, PACK], F32, name="gam", align_bytes=ALIGN)
        nc.sync.dma_start(out=gam[:], in_=gamma.rearrange("(p t) o -> p (t o)", t=PACK))
        w2_codes = keep.tile([P, N], U32, name="w2_codes", align_bytes=DMA_ALIGN)
        nc.sync.dma_start(out=w2_codes[:].bitcast(I32), in_=w2_words[0].rearrange("p n j -> p (n j)").bitcast(I32))

        joined = [keep.tile([P, S, PACK], BF16, name=f"x_joined_{g}", align_bytes=ALIGN) for g in range(PASSES)]
        first_codes = keep.tile([P, S], U32, name="x_codes_0", align_bytes=ALIGN)
        first_scales = keep.tile([P, S], U8, name="x_scales_0", align_bytes=ALIGN)
        second_codes = {}
        second_scales = {}

        def quantise_points(g, n, codes, scales):
            values = joined[g][:, n * HALF : (n + 1) * HALF, :].rearrange("p n j -> p (n j)")
            nc.vector.quantize_mx(out=codes.bitcast(FP8X4), scales=scales, in_=values)

        def quantise_second_pass(n, tag):
            second_codes[n] = keep.tile([P, HALF], U32, name=f"x_codes_1_{n}", tag=tag, align_bytes=ALIGN)
            second_scales[n] = keep.tile([P, HALF], U8, name=f"x_scales_1_{n}", align_bytes=ALIGN)
            quantise_points(1, n, second_codes[n][:], second_scales[n][:])

        for g in range(PASSES):
            found = keep.tile([P, PACK, S], F32, name=f"x_found_{g}", align_bytes=ALIGN)
            for u in range(2):
                for a, b in [(0, HALF), (HALF, S)] if (g, u) == (1, 1) else [(0, S)]:
                    part = offsets[:, a // 16 : b // 16]
                    for r in range(2):
                        copy_floats(r == 0, found[:, 2 * u + r, a:b], x_raw[g, u][:, r, :].indirect(part))
            cut = JOIN_ON_VECTOR[g]
            interleave(copy_floats, True, joined[g][:, 0:HALF, :], found[:, :, 0:HALF])
            if cut > HALF:
                interleave(copy_floats, True, joined[g][:, HALF:cut, :], found[:, :, HALF:cut])
            interleave(copy_floats, False, joined[g][:, cut:S, :], found[:, :, cut:S])
            if g == 0:
                for n in range(2):
                    cols = slice(n * HALF, (n + 1) * HALF)
                    quantise_points(0, n, first_codes[:, cols], first_scales[:, cols])

        dealt = {}
        w_codes = {}
        w_scales = {}

        def deal_weights(g, u):
            cut = W_ON_SCALAR[g][u]
            dealt[g, u] = keep.tile([P, 2, P, PACK], BF16, name=f"w_dealt_{g}_{u}", align_bytes=ALIGN)
            dst = dealt[g, u][:].rearrange("p s m j -> p m j s")
            src = w_raw[g][:].rearrange("p j (m t) -> p m j t", t=PACK)[:, :, :, 2 * u : 2 * u + 2]
            copy_floats(False, dst[:, 0:cut], src[:, 0:cut])
            copy_floats(True, dst[:, cut:P], src[:, cut:P])

        def quantise_weights(g, u, s0, s1):
            codes = keep.tile([P, (s1 - s0) * P], U32, name=f"w_codes_{g}_{u}_{s0}", align_bytes=ALIGN)
            scales = keep.tile([P, (s1 - s0) * P], U8, name=f"w_scales_{g}_{u}_{s0}", align_bytes=ALIGN)
            nc.vector.quantize_mx(out=codes[:].bitcast(FP8X4), scales=scales[:], in_=dealt[g, u][:, s0:s1].rearrange("p s m j -> p (s m j)"))
            for s in range(s0, s1):
                w_codes[g, 2 * u + s] = codes[:, (s - s0) * P : (s - s0 + 1) * P]
                w_scales[g, 2 * u + s] = scales[:, (s - s0) * P : (s - s0 + 1) * P]

        quantise_second_pass(0, "x_codes_1_0")
        deal_weights(0, 0)
        quantise_weights(0, 0, 0, 2)
        deal_weights(0, 1)
        quantise_second_pass(1, "w_dealt_0_0")
        quantise_weights(0, 1, 0, 2)
        for u in range(2):
            deal_weights(1, u)
        for t in range(PACK):
            quantise_weights(1, t // 2, t % 2, t % 2 + 1)

        def warm_up(tag, codes, scales):
            idle = psum.tile([NARROW, S], F32, name="idle_" + tag, tag=tag)
            for r in range(2):
                nc.tensor.matmul_mx(
                    out=idle[:],
                    lhsT=codes[:, r * P : r * P + NARROW].bitcast(FP8X4),
                    lhsT_scale=scales[:, r * P : r * P + NARROW],
                    rhs=first_codes[:].bitcast(FP8X4),
                    rhs_scale=first_scales[:],
                    start=True,
                    stop=True,
                )

        warm_up("acc_0", first_codes, w2_plane)
        for q in range(1, 4):
            load_scale_rows(q)

        spans = {t: [(0, S)] if t == SUMMED else [(0, HALF), (HALF, S)] for t in range(PACK)}
        banks = {(t, a): psum.tile([P, b - a], F32, name=f"h_{t}_{a}") for t in range(PACK) for a, b in spans[t]}
        for t in range(PACK):
            for a, b in spans[t]:
                nc.tensor.matmul_mx(
                    out=banks[t, a][:],
                    lhsT=w_codes[0, t].bitcast(FP8X4),
                    lhsT_scale=w_scales[0, t],
                    rhs=first_codes[:, a:b].bitcast(FP8X4),
                    rhs_scale=first_scales[:, a:b],
                    start=True,
                    stop=False,
                )
        for t in range(PACK):
            for n in range(2):
                nc.tensor.matmul_mx(
                    out=banks[t, 0][:, n * HALF : (n + 1) * HALF] if t == SUMMED else banks[t, n * HALF][:],
                    lhsT=w_codes[1, t].bitcast(FP8X4),
                    lhsT_scale=w_scales[1, t],
                    rhs=second_codes[n][:].bitcast(FP8X4),
                    rhs_scale=second_scales[n][:],
                    start=False,
                    stop=t != SUMMED or n == 1,
                )

        stats = {t: keep.tile([P, 2, 6], F32, name=f"stats_{t}") for t in range(PACK) if t != SUMMED}
        rstd = keep.tile([P, PACK], F32, name="rstd")
        factors = [keep.tile([P, 2], F32, name=f"factors_{t}") for t in range(PACK)]
        minus_gam = keep.tile([P, PACK], F32, name="minus_gam")
        h_copy = keep.tile([P, S], F32, name="h_copy")
        z_halves = [keep.tile([P, PACK, HALF], BF16, name=f"z_planes_{n}", align_bytes=ALIGN) for n in range(2)]

        def z_plane(t, a, b):
            return z_halves[a // HALF][:, t, a % HALF : a % HALF + b - a]

        z_joined = [keep.tile([P, QUARTER, PACK], BF16, name=f"z_joined_{c}", align_bytes=ALIGN) for c in range(4)]
        nc.scalar.activation(out=minus_gam[:], in_=gam[:], func=ACT.Copy, scale=-1.0)

        def statistics(t, n):
            nc.vector.bn_stats(out=stats[t][:, n, :], in_=banks[t, n * HALF][:])

        def close_statistics(t):
            nc.vector.bn_aggr(out=moments[:, t, 1:3], in_=stats[t][:].rearrange("p n s -> p (n s)"))
            nc.scalar.activation(out=rstd[:, t : t + 1], in_=moments[:, t, 2:3], func=ACT.Abs_reciprocal_sqrt, bias=EPS)

        def make_factors(t):
            signed_gam = gam if t == SUMMED else minus_gam
            nc.vector.tensor_scalar(
                out=factors[t][:],
                in0=moments[:, t, 0:2],
                scalar1=rstd[:, t : t + 1],
                scalar2=signed_gam[:, t : t + 1],
                op0=ALU.mult,
                op1=ALU.mult,
            )

        def normalise(on_vector, t, a, b, values):
            scale, bias = factors[t][:, 0:1], factors[t][:, 1:2]
            if on_vector:
                nc.vector.tensor_scalar(out=z_plane(t, a, b), in0=values, scalar1=scale, scalar2=bias, op0=ALU.mult, op1=ALU.add)
            else:
                nc.scalar.activation(out=z_plane(t, a, b), in_=values, func=ACT.Identity, scale=scale, bias=bias)

        h_scaled = keep.tile([P, S], F32, name="h_scaled")
        scaled_mean = keep.tile([P, 1], F32, name="scaled_mean")

        def copy_scaled(n):
            nc.scalar.activation(
                out=h_scaled[:, 0:QUARTER], in_=banks[LAST, 0][:, 0:QUARTER], func=ACT.Copy, scale=gam[:, LAST : LAST + 1]
            )

        def normalise_last(a, b):
            nc.vector.tensor_scalar(
                out=z_plane(LAST, a, b),
                in0=h_scaled[:, a:b],
                scalar1=scaled_mean[:],
                scalar2=rstd[:, LAST : LAST + 1],
                op0=ALU.subtract,
                op1=ALU.mult,
            )

        statistics(0, 0)
        statistics(0, 1)
        nc.scalar.activation(out=h_copy[:], in_=banks[SUMMED, 0][:], func=ACT.Copy, scale=-1.0 / S, accum_out=moments[:, SUMMED, 1:2])
        statistics(2, 0)
        close_statistics(0)
        statistics(2, 1)
        nc.scalar.activation(
            out=h_scaled[:],
            in_=banks[SUMMED, 0][:],
            func=ACT.Square,
            bias=moments[:, SUMMED, 1:2],
            accum_out=moments[:, SUMMED, 2:3],
        )
        statistics(LAST, 0)
        make_factors(0)
        close_statistics(2)
        statistics(LAST, 1)
        nc.scalar.activation(
            out=rstd[:, SUMMED : SUMMED + 1], in_=moments[:, SUMMED, 2:3], func=ACT.Abs_reciprocal_sqrt, scale=1.0 / S, bias=EPS
        )
        make_factors(2)
        copy_scaled(0)
        normalise(False, 0, 0, HALF, banks[0, 0][:])
        warm_up("h_0_0", second_codes[0], second_scales[0])
        close_statistics(LAST)
        make_factors(SUMMED)
        normalise(True, 2, 0, HALF, banks[2, 0][:])
        nc.vector.tensor_scalar(out=scaled_mean[:], in0=moments[:, LAST, 1:2], scalar1=gam[:, LAST : LAST + 1], scalar2=None, op0=ALU.mult)
        normalise(True, SUMMED, 0, HALF, h_copy[:, 0:HALF])
        normalise(False, 0, HALF, S, banks[0, HALF][:])
        make_factors(LAST)
        normalise_last(0, QUARTER)
        normalise(True, LAST, QUARTER, HALF, banks[LAST, 0][:, QUARTER:HALF])
        normalise(False, 2, HALF, S, banks[2, HALF][:])
        normalise(True, SUMMED, HALF, S, h_copy[:, HALF:S])
        normalise(False, LAST, HALF, 3 * QUARTER, banks[LAST, HALF][:, 0:QUARTER])
        normalise(False, LAST, 3 * QUARTER, S, banks[LAST, HALF][:, QUARTER:HALF])

        def join_z(on_vector, c, a, b):
            interleave(copy_bits, on_vector, z_joined[c][:, a:b, :], z_halves[c // 2][:, :, c % 2 * QUARTER + a : c % 2 * QUARTER + b])

        banks_of = {0: ("acc_0", "h_1_0"), 1: ("h_3_0", "h_0_0"), 2: ("h_2_0", "h_0_256"), 3: ("h_2_256", "h_3_256")}
        out_rows = out.rearrange("(r p) n -> p r n", p=P)
        result = keep.tile([P, 2, S], F32, name="result", align_bytes=DMA_ALIGN)
        stores = {0: (0, QUARTER), 1: (QUARTER, HALF), 3: (HALF, S)}

        def second_product(c):
            cols = slice(c * QUARTER, (c + 1) * QUARTER)
            z_codes = keep.tile([P, QUARTER], U32, name=f"z_codes_{c}", align_bytes=ALIGN)
            z_scales = keep.tile([P, QUARTER], U8, name=f"z_scales_{c}", align_bytes=ALIGN)
            nc.vector.quantize_mx(out=z_codes[:].bitcast(FP8X4), scales=z_scales[:], in_=z_joined[c][:].rearrange("p n t -> p (n t)"))
            sums = [psum.tile([P, QUARTER], F32, name=f"acc_{c}_{r}", tag=banks_of[c][r])[:] for r in range(2)]
            for r in range(2):
                nc.tensor.matmul_mx(
                    out=sums[r],
                    lhsT=w2_codes[:, r * P : (r + 1) * P].bitcast(FP8X4),
                    lhsT_scale=w2_plane[:, r * P : (r + 1) * P],
                    rhs=z_codes[:].bitcast(FP8X4),
                    rhs_scale=z_scales[:],
                    start=True,
                    stop=True,
                )
            for r in range(2):
                copy_floats(r == 1 and c > 0, result[:, r, cols], sums[r])
            if c in stores:
                a, b = stores[c]
                nc.sync.dma_start(out=out_rows[:, :, a:b], in_=result[:, :, a:b])

        join_z(True, 0, 0, QUARTER)
        join_z(False, 2, 0, QUARTER)
        join_z(True, 1, 0, QUARTER)
        join_z(False, 3, 0, LAST_JOIN_ON_SCALAR)
        second_product(0)
        join_z(True, 3, LAST_JOIN_ON_SCALAR, QUARTER)
        for c in range(1, 4):
            second_product(c)
